import numpy as np
import ml_dtypes


def mxq(x, axis, fmt="e4m3"):
    dtype, down = {"e4m3": (ml_dtypes.float8_e4m3fn, 7), "e5m2": (ml_dtypes.float8_e5m2, 14)}[fmt]
    v = np.moveaxis(np.asarray(x, np.float32).astype(ml_dtypes.bfloat16).astype(np.float64), axis, -1)
    blocks = v.reshape(v.shape[:-1] + (-1, 32))
    amax = np.abs(blocks).max(-1, keepdims=True)
    byte = np.maximum(np.where(amax > 0, np.frexp(amax)[1] - 1 + 127, 0) - down, 1)
    scale = np.exp2(byte - 127.0)
    codes = (blocks / scale).astype(np.float32).astype(dtype).astype(np.float64)
    return np.moveaxis((codes * scale).reshape(v.shape), -1, axis)


WIDE = False


def mx_kscale(k):
    if not WIDE:
        return np.ones(k)
    levels = np.array([10, -10, 5, -5, 0])
    if k % 512:
        return np.exp2(np.random.permutation(np.resize(levels, k // 32))).repeat(32)
    a = np.empty((k // 512, 16))
    for p in range(k // 512):
        a[p, :8] = np.random.permutation(np.resize(levels, 8))
        for g in range(8):
            far = levels[np.abs(levels - a[p, g]) >= 10]
            a[p, g + 8] = far[np.random.randint(len(far))]
    return np.exp2(a.ravel()).repeat(32)


BF16 = ml_dtypes.bfloat16


def bf(x):
    return np.asarray(x, np.float32).astype(BF16)


def f64(x):
    return np.asarray(x).astype(np.float64)


E2M1 = np.array([0.0, 0.5, 1.0, 1.5, 2.0, 3.0, 4.0, 6.0, -0.0, -0.5, -1.0, -1.5, -2.0, -3.0, -4.0, -6.0])


def pack_weight(w, fmt):
    k, n = w.shape
    w = f64(bf(w)).reshape(k // 32, 32, n)
    amax = np.abs(w).max(1)
    if fmt == "e4m3":
        byte = np.frexp(amax)[1] - 1 + 127 - 7
    else:
        mant, ex = np.frexp(amax / 6.0)
        byte = np.where(mant > 0.5, ex, ex - 1) + 127
    byte = np.clip(np.where(amax > 0, byte, 1), 1, 254)
    scaled = (w * np.exp2(127.0 - byte)[:, None, :]).reshape(k, n).astype(np.float32)
    by_word = np.ascontiguousarray(scaled.reshape(k // 512, 128, 4, n).transpose(0, 1, 3, 2))
    if fmt == "e4m3":
        words = by_word.astype(ml_dtypes.float8_e4m3fn).view(np.uint8)
    else:
        c = by_word.astype(ml_dtypes.float4_e2m1fn).view(np.uint8) & 0xF
        words = c[..., 0::2] | (c[..., 1::2] << 4)
    return np.ascontiguousarray(words), np.ascontiguousarray(byte.astype(np.uint8).reshape(k // 512, 16, n))


def unpack_weight(words, scales, fmt):
    g, p, n, _ = words.shape
    if fmt == "e4m3":
        vals = np.ascontiguousarray(words).view(ml_dtypes.float8_e4m3fn).astype(np.float64)
    else:
        nib = np.empty((g, p, n, 4), np.uint8)
        nib[..., 0::2] = words & 0xF
        nib[..., 1::2] = words >> 4
        vals = E2M1[nib]
    vals = vals * np.repeat(np.exp2(scales.astype(np.float64) - 127.0), 8, axis=1)[..., None]
    return vals.transpose(0, 1, 3, 2).reshape(g * 512, n)
def pack4(w):
    words, scales = pack_weight(w, "e2m1")
    return words.reshape(words.shape[0], 128, -1), scales


def unpack4(words, scales):
    return unpack_weight(words.reshape(words.shape[0], 128, -1, 2), scales, "e2m1")


def planes(Y):
    n, m = Y.shape
    b = f64(bf(Y)).reshape(n // 32, 32, m)
    amax = np.abs(b).max(1)
    byte = np.clip(np.where(amax > 0, np.frexp(amax)[1] - 1 + 127 - 7, 1), 1, 254)
    codes = (b * np.exp2(127.0 - byte)[:, None, :]).reshape(n, m).astype(np.float32).astype(ml_dtypes.float8_e4m3fn).view(np.uint8)
    words = codes.reshape(n // 512, 128, 4, m).transpose(0, 1, 3, 2)
    return np.ascontiguousarray(words), np.ascontiguousarray(byte.astype(np.uint8).reshape(n // 512, 16, m))


G, P, B, V, O = 4, 512, 1024, 1536, 512
ALPHA, BETA, FRACTIONS = 0.15, 0.03, 5.0

def setup_inputs():
    noise = np.random.randn
    s = mx_kscale(G * B).reshape(G, B)
    t = mx_kscale(G * V).reshape(G, V)
    x = 1.2 * np.exp(0.7 * noise(G, P, B)) * (0.5 + np.random.rand(G, P, 1))
    dose = np.exp(1.2 * noise(G, B, V))
    dose = dose / dose.sum(axis=1, keepdims=True) * np.exp(0.4 * noise(G, 1, V))
    member = np.exp(1.2 * noise(G, V, O))
    member = member / member.sum(axis=1, keepdims=True)
    dose_words, dose_scales = pack4((dose / s[:, :, None]).reshape(G * B, V))
    member_words, member_scales = pack4((member / t[:, :, None]).reshape(G * V, O))
    return {"x": bf(x * s[:, None, :]), "dose_words": dose_words, "dose_scales": dose_scales,
            "density": bf(np.exp(0.5 * noise(G, V)) * t),
            "member_words": member_words, "member_scales": member_scales,
            "burden": bf(3.0 * np.exp(0.8 * noise(G, O))),
            "regrowth": bf(np.exp(0.3 * np.abs(noise(G, P))))}

def reference(x, dose_words, dose_scales, density, member_words, member_scales, burden, regrowth):
    A = unpack4(dose_words, dose_scales).reshape(G, B, V)
    C = unpack4(member_words, member_scales).reshape(G, V, O)
    D = mxq(f64(x), 2, "e4m3") @ A
    H = f64(density)[:, None, :] * np.exp(-FRACTIONS * (ALPHA * D + BETA * D * D))
    y = (mxq(H, 2, "e4m3") @ C) * f64(burden)[:, None, :] * f64(regrowth)[:, :, None]
    Y = y.reshape(G * P, O).T
    words, scales = planes(Y)
    return y, words, scales

@@ -1,0 +1,448 @@
+from contextlib import ExitStack
+
+import concourse.mybir as mybir
+from concourse.masks import make_identity
+
+G, PLANS, B, V, O = 4, 512, 1024, 1536, 512
+FLOPS = 2 * G * PLANS * (B * V + V * O)
+
+F32 = mybir.dt.float32
+BF16 = mybir.dt.bfloat16
+I32 = mybir.dt.int32
+U32 = mybir.dt.uint32
+U8 = mybir.dt.uint8
+FP8X4 = mybir.dt.float8_e4m3fn_x4
+FP4X4 = mybir.dt.float4_e2m1fn_x4
+ACT = mybir.ActivationFunctionType
+ALU = mybir.AluOpType
+
+P = 128
+KP = 512
+TILES = G * PLANS // P
+TPP = PLANS // P
+GB = B // KP
+GV = V // KP
+
+X_LEAD = 2
+H_T_LAG = 2
+S2_LAG = 4
+Y_T_LAG = 5
+LAST = TILES - 1
+SPARE_FROM = 12
+YC_ENGINE = "gpsimd"
+YC_TAIL = "scalar"
+EVERY = 4
+LATE = 16
+
+
+def tile_fractionated_clonogen_survival_k7_kernel(
+    tc, x, dose_words, dose_scales, density, member_words, member_scales, burden, regrowth, out_0, out_1, out_2
+):
+    nc = tc.nc
+    x_rows = x.rearrange("j r k -> (j r) k")
+    y_rows = out_0.rearrange("j r o -> (j r) o")
+    out_codes = out_1[0].rearrange("p m t -> p (m t)").bitcast(I32)
+    out_scales = out_2[0].bitcast(I32)
+
+    with ExitStack() as ctx:
+        keep = ctx.enter_context(tc.tile_pool(name="keep", bufs=1))
+        work = ctx.enter_context(tc.tile_pool(name="work", bufs=5))
+        d_psum = ctx.enter_context(tc.psum_pool(name="d_psum", bufs=3))
+        t_psum = ctx.enter_context(tc.psum_pool(name="t_psum", bufs=4))
+        y_psum = ctx.enter_context(tc.psum_pool(name="y_psum", bufs=1))
+        ctx.enter_context(tc.manual_schedule())
+
+        x_sb = keep.tile([P, TILES, B], BF16, align_bytes=64)
+        a_words = keep.tile([P, G * GB, 2 * V], U8, align_bytes=64)
+        a_scales = keep.tile([P, G * GB, V], U8, align_bytes=64)
+        c_words = keep.tile([P, G * GV, 2 * O], U8, align_bytes=64)
+        c_scales = keep.tile([P, G * GV, O], U8, align_bytes=64)
+        dens = keep.tile([P, G, V], BF16, align_bytes=64)
+        burd = keep.tile([P, G * O], BF16, align_bytes=64)
+        y_sb = keep.tile([P, TILES, O], F32, align_bytes=64)
+        y_codes = keep.tile([P, TILES * P], U32, align_bytes=64)
+        y_scales = keep.tile([P, TILES * P], U8, align_bytes=64)
+        ident = keep.tile([P, P], F32)
+        reg_raw = keep.tile([TILES, P], BF16)
+        reg_rows = keep.tile([P, P], F32)
+        reg = keep.tile([P, TILES], F32)
+        warm = keep.tile([P, 8], F32)
+
+        def zero_plane(plane):
+            nc.vector.memset(plane.rearrange("p g n -> p (g n)").bitcast(I32), 0)
+
+        def load_scales(plane, src, g0, g1):
+            for q in range(4):
+                nc.sync.dma_start(
+                    out=plane[32 * q : 32 * q + 4, g0:g1, :].bitcast(I32),
+                    in_=src[g0:g1, 4 * q : 4 * q + 4, :].rearrange("g r n -> r g n").bitcast(I32),
+                )
+
+        def load_words(tile, src, g0, g1, cols=slice(None)):
+            nc.sync.dma_start(
+                out=tile[:, g0:g1, cols].bitcast(I32), in_=src[g0:g1, :, cols].rearrange("g p n -> p g n").bitcast(I32)
+            )
+
+        def load_x(i0, i1):
+            nc.sync.dma_start(
+                out=x_sb[:, i0:i1, :], in_=x_rows[i0 * P : i1 * P, :].rearrange("(i p) k -> p i k", p=P)
+            )
+
+        def load_density(j):
+            nc.sync.dma_start(out=dens[:, j, :], in_=density[j].partition_broadcast(P))
+
+        make_identity(nc, ident[:])
+        zero_plane(a_scales[:, 0:GB, :])
+        nc.vector.memset(warm[:], 0.0)
+        nc.scalar.activation(out=warm[:, 4:5], in_=warm[:, 0:1], func=ACT.Exp)
+        load_x(0, 1)
+        load_scales(a_scales, dose_scales, 0, GB)
+        load_words(a_words, dose_words, 0, GB, slice(0, 2 * KP))
+        load_words(a_words, dose_words, 0, GB, slice(2 * KP, 2 * V))
+        load_x(1, 2)
+        zero_plane(c_scales[:])
+        zero_plane(a_scales[:, GB:, :])
+        nc.gpsimd.memset(reg_rows[:], 0.0)
+        load_density(0)
+        nc.sync.dma_start(out=reg_raw[:], in_=regrowth.rearrange("j (m p) -> (j m) p", p=P))
+        load_x(2, TPP)
+        load_scales(c_scales, member_scales, 0, G * GV)
+        load_scales(a_scales, dose_scales, GB, G * GB)
+        load_words(c_words, member_words, 0, GV)
+        nc.sync.dma_start(out=burd[:], in_=burden.rearrange("j o -> (j o)").partition_broadcast(P))
+        for j in range(1, G):
+            load_x(j * TPP, (j + 1) * TPP)
+            load_words(a_words, dose_words, j * GB, (j + 1) * GB)
+            load_density(j)
+            load_words(c_words, member_words, j * GV, (j + 1) * GV)
+        nc.gpsimd.tensor_copy(out=reg_rows[0:TILES, :], in_=reg_raw[:])
+
+        def live(i):
+            return 0 <= i < TILES
+
+        x_bank, x_grouped, x_q = {}, {}, {}
+        d_banks, squares, expo, h_bf, h_grouped, h_q = {}, {}, {}, {}, {}, {}
+        y_banks, y_bf = {}, {}
+        h_src, y_src, y_grouped = {}, {}, {}
+
+        def new_t_bank():
+            return t_psum.tile([P, KP], F32, name="t_bank")
+
+        def evacuate(on_scalar, dst_words, bank):
+            src = bank.rearrange("p (a u c) -> p a c u", u=2, c=P)
+            dst = dst_words.rearrange("p (a c u) -> p a c u", u=2, c=P)
+            if on_scalar:
+                nc.scalar.copy(out=dst, in_=src)
+            else:
+                nc.vector.tensor_copy(out=dst, in_=src)
+
+        def x_transpose(i):
+            x_bank[i] = new_t_bank()
+            words = x_sb[:, i, :].bitcast(F32)
+            for g in range(GB):
+                for u in range(2):
+                    c0 = (2 * g + u) * P
+                    nc.tensor.transpose(
+                        x_bank[i][:, c0 : c0 + P], words[:, 256 * g + u : 256 * (g + 1) : 2], ident[:]
+                    )
+
+        def x_evacuate(i, on_scalar):
+            x_grouped[i] = work.tile([P, B], BF16, align_bytes=64, name="xg", bufs=3)
+            evacuate(on_scalar, x_grouped[i][:].bitcast(F32), x_bank[i][:])
+
+        def x_quantize(i):
+            xc = work.tile([P, GB * P], U32, align_bytes=64, name="xc")
+            xs = work.tile([P, GB * P], U8, align_bytes=64, name="xs")
+            x_q[i] = (xc, xs)
+            nc.vector.quantize_mx(out=xc[:].bitcast(FP8X4), scales=xs[:], in_=x_grouped[i][:])
+
+        def dose(i, vg):
+            j = i // TPP
+            xc, xs = x_q[i]
+            d_banks[i, vg] = d_psum.tile([P, KP], F32, name="d_bank")
+            for g in range(GB):
+                nc.tensor.matmul_mx(
+                    out=d_banks[i, vg][:],
+                    lhsT=xc[:, g * P : (g + 1) * P].bitcast(FP8X4),
+                    lhsT_scale=xs[:, g * P : (g + 1) * P],
+                    rhs=a_words[:, j * GB + g, vg * 2 * KP : (vg + 1) * 2 * KP].bitcast(FP4X4),
+                    rhs_scale=a_scales[:, j * GB + g, vg * KP : (vg + 1) * KP],
+                    start=(g == 0),
+                    stop=(g == GB - 1),
+                )
+
+        def square(i, vg):
+            if vg == 0:
+                squares[i] = work.tile([P, 2, GV, 256], F32, name="sq", bufs=2)
+            nc.scalar.activation(
+                out=squares[i][:, :, vg, :].rearrange("q u (w e) -> q u w e", e=2),
+                in_=d_banks[i, vg][:].rearrange("q (w u e) -> q u w e", u=2, e=2),
+                func=ACT.Square,
+                bias=2.5,
+            )
+
+        def exponential(i, v0, v1):
+            if v0 == 0:
+                expo[i] = work.tile([P, 2, GV, 256], F32, name="ex", bufs=3)
+            nc.scalar.activation(
+                out=expo[i][:, :, v0:v1, :], in_=squares[i][:, :, v0:v1, :], func=ACT.Exp, bias=0.9375, scale=-0.15
+            )
+
+        def times_density(i, v0, v1):
+            if v0 == 0:
+                h_bf[i] = work.tile([P, 2, GV, 256], BF16, align_bytes=64, name="hb", bufs=4)
+            nc.vector.tensor_tensor(
+                out=h_bf[i][:, :, v0:v1, :].rearrange("q u g (w e) -> q u (g w) e", e=2),
+                in0=expo[i][:, :, v0:v1, :].rearrange("q u g (w e) -> q u (g w) e", e=2),
+                in1=dens[:, i // TPP, v0 * KP : v1 * KP].rearrange("q (w u e) -> q u w e", u=2, e=2),
+                op=ALU.mult,
+            )
+
+        def h_transpose(i, vg, bank, slot):
+            h_src[i, vg] = (bank, slot)
+            for u in range(2):
+                c0 = (2 * slot + u) * P
+                nc.tensor.transpose(bank[:, c0 : c0 + P], h_bf[i][:, u, vg, :].bitcast(F32), ident[:])
+
+        def y_transpose(i, bank, slot):
+            y_src[i] = (bank, slot)
+            for u in range(2):
+                c0 = (2 * slot + u) * P
+                nc.tensor.transpose(bank[:, c0 : c0 + P], y_bf[i][:, u, :].bitcast(F32), ident[:])
+
+        def new_grouped():
+            return work.tile([P, V + O], BF16, align_bytes=64, name="hg")
+
+        def h_quantize(i, v0, v1):
+            if v0 == 0:
+                hc = work.tile([P, GV * P], U32, align_bytes=64, name="hc")
+                hs = work.tile([P, GV * P], U8, align_bytes=64, name="hs")
+                h_q[i] = (hc, hs)
+            hc, hs = h_q[i]
+            nc.vector.quantize_mx(
+                out=hc[:, v0 * P : v1 * P].bitcast(FP8X4),
+                scales=hs[:, v0 * P : v1 * P],
+                in_=h_grouped[i][:, v0 * KP : v1 * KP],
+            )
+
+        def average(i, v0, v1):
+            j = i // TPP
+            hc, hs = h_q[i]
+            if v0 == 0:
+                if i >= SPARE_FROM:
+                    y_banks[i] = d_psum.tile([P, O], F32, name="d_bank")
+                else:
+                    y_banks[i] = y_psum.tile([P, O], F32, name="y_bank")
+            for vg in range(v0, v1):
+                nc.tensor.matmul_mx(
+                    out=y_banks[i][:],
+                    lhsT=hc[:, vg * P : (vg + 1) * P].bitcast(FP8X4),
+                    lhsT_scale=hs[:, vg * P : (vg + 1) * P],
+                    rhs=c_words[:, j * GV + vg, :].bitcast(FP4X4),
+                    rhs_scale=c_scales[:, j * GV + vg, :],
+                    start=(vg == 0),
+                    stop=(vg == GV - 1),
+                )
+
+        def y_scale(i):
+            j = i // TPP
+            nc.vector.scalar_tensor_tensor(
+                out=y_sb[:, i, :],
+                in0=y_banks[i][:],
+                scalar=reg[:, i : i + 1],
+                in1=burd[:, j * O : (j + 1) * O],
+                op0=ALU.mult,
+                op1=ALU.mult,
+            )
+            nc.sync.dma_start(out=y_rows[i * P : (i + 1) * P, :], in_=y_sb[:, i, :])
+
+        def y_round(i, engine):
+            y_bf[i] = work.tile([P, 2, 256], BF16, align_bytes=64, name="yb")
+            dst = y_bf[i][:].rearrange("q u (w e) -> q u w e", e=2)
+            src = y_sb[:, i, :].rearrange("q (w u e) -> q u w e", u=2, e=2)
+            if engine == "gpsimd":
+                nc.gpsimd.tensor_scalar(out=dst, in0=src, scalar1=1.0, scalar2=1.0, op0=ALU.mult, op1=ALU.mult)
+            elif engine == "scalar":
+                nc.scalar.copy(out=dst, in_=src)
+            else:
+                nc.vector.tensor_copy(out=dst, in_=src)
+
+        def y_scale_round(i):
+            j = i // TPP
+            y_bf[i] = work.tile([P, 2, 256], BF16, align_bytes=64, name="yb")
+            for u in range(2):
+                nc.vector.scalar_tensor_tensor(
+                    out=y_bf[i][:, u, :].rearrange("q (w e) -> q w e", e=2),
+                    in0=y_banks[i][:].rearrange("q (w u e) -> q u w e", u=2, e=2)[:, u],
+                    scalar=reg[:, i : i + 1],
+                    in1=burd[:, j * O : (j + 1) * O].rearrange("q (w u e) -> q u w e", u=2, e=2)[:, u],
+                    op0=ALU.mult,
+                    op1=ALU.mult,
+                )
+
+        def h_evacuate(i, v0, v1, on_scalar):
+            if i not in h_grouped:
+                h_grouped[i] = work.tile([P, V + O], BF16, align_bytes=64, name="hg")
+            bank, slot = h_src[i, v0]
+            n = (v1 - v0) * 256
+            evacuate(
+                on_scalar, h_grouped[i][:].bitcast(F32)[:, v0 * 256 : v1 * 256], bank[:, slot * 256 : slot * 256 + n]
+            )
+
+        def y_evacuate(i, on_scalar):
+            y_grouped[i] = work.tile([P, V + O], BF16, align_bytes=64, name="hg")
+            bank, slot = y_src[i]
+            evacuate(on_scalar, y_grouped[i][:].bitcast(F32)[:, 768:1024], bank[:, slot * 256 : slot * 256 + 256])
+
+        def store_planes(i0, i1):
+            cols = slice(i0 * P, i1 * P)
+            nc.sync.dma_start(out=out_codes[:, cols], in_=y_codes[:, cols].bitcast(I32))
+
+        def store_scales(i0, i1, queues):
+            for q in range(4):
+                queues[q % len(queues)].dma_start(
+                    out=out_scales[4 * q : 4 * q + 4, i0 * 32 : i1 * 32],
+                    in_=y_scales[32 * q : 32 * q + 4, i0 * P : i1 * P].bitcast(I32),
+                )
+
+        def y_quantize(i):
+            cols = slice(i * P, (i + 1) * P)
+            nc.vector.quantize_mx(
+                out=y_codes[:, cols].bitcast(FP8X4), scales=y_scales[:, cols], in_=y_grouped[i][:, V : V + O]
+            )
+
+        x_transpose(0)
+        x_evacuate(0, False)
+        x_quantize(0)
+        a_bank, b_bank = {}, {}
+        reg_bank = None
+        for s in range(0, TILES):
+            ix, ih, iy = s - 1 + X_LEAD, s - 1 - H_T_LAG, s - 1 - Y_T_LAG
+            i2 = s - S2_LAG
+            late = s >= LATE
+            if live(ih):
+                hg = new_grouped()
+                h_grouped[ih] = hg
+                y_grouped[iy] = hg
+                words = hg[:].bitcast(F32)
+                if not late:
+                    evacuate(True, words[:, 0:512], a_bank[s - 1][:])
+                hi = 512 if live(iy) else 256
+                b_on_scalar = s % EVERY == 0 and not late
+                if b_on_scalar:
+                    evacuate(True, words[:, 512 : 512 + hi], b_bank[s - 1][:, 0:hi])
+            for vg in range(GV):
+                dose(s, vg)
+                if s == 0 and vg == 0:
+                    x_transpose(1)
+                square(s, vg)
+                if s == LAST and vg > 0:
+                    exponential(s, vg - 1, vg)
+            if live(i2 - 1):
+                y_scale(i2 - 1)
+                y_round(i2 - 1, YC_ENGINE)
+            if live(i2):
+                average(i2, 0, GV)
+            if live(ix):
+                x_evacuate(ix, False)
+            if s == 1:
+                nc.vector.tensor_copy(out=reg[:], in_=reg_bank[:, 0:TILES])
+            if live(ih):
+                if not b_on_scalar:
+                    evacuate(False, words[:, 512 : 512 + hi], b_bank[s - 1][:, 0:hi])
+                if late:
+                    evacuate(False, words[:, 0:512], a_bank[s - 1][:])
+            if s == LAST:
+                exponential(s, GV - 1, GV)
+            else:
+                exponential(s, 0, 2)
+                exponential(s, 2, 3)
+            if live(ix):
+                x_quantize(ix)
+            if live(s - 1):
+                times_density(s - 1, 0, GV)
+            if live(iy):
+                y_quantize(iy)
+                if iy % TPP == TPP - 1:
+                    store_planes(iy + 1 - TPP, iy + 1)
+            if live(ih):
+                h_quantize(ih, 0, 2)
+                h_quantize(ih, 2, 3)
+
+            tx, th, ty = s + X_LEAD, s - H_T_LAG, s - Y_T_LAG
+            if live(tx):
+                x_transpose(tx)
+            if s == 0:
+                reg_bank = new_t_bank()
+                nc.tensor.transpose(reg_bank[:, 0:P], reg_rows[:], ident[:])
+            if live(th):
+                a_bank[s] = new_t_bank()
+                b_bank[s] = new_t_bank()
+            if live(ty):
+                y_transpose(ty, b_bank[s], 1)
+            if live(th):
+                for vg in range(GV):
+                    h_transpose(th, vg, a_bank[s] if vg < 2 else b_bank[s], vg % 2)
+
+        times_density(15, 0, 1)
+        average(12, 0, GV)
+        bank0, bank1 = new_t_bank(), None
+        h_transpose(14, 0, bank0, 0)
+        h_transpose(14, 1, bank0, 1)
+        y_scale(11)
+        y_round(11, YC_ENGINE)
+        h_evacuate(13, 0, 2, True)
+        times_density(15, 1, 2)
+        h_evacuate(13, 2, 3, True)
+        bank1 = new_t_bank()
+        h_transpose(14, 2, bank1, 0)
+        h_transpose(15, 0, bank1, 1)
+        y_evacuate(10, True)
+        times_density(15, 2, 3)
+        h_evacuate(14, 0, 2, True)
+        bank2 = new_t_bank()
+        h_transpose(15, 1, bank2, 0)
+        h_transpose(15, 2, bank2, 1)
+        h_quantize(13, 0, 2)
+        h_quantize(13, 2, 3)
+        average(13, 0, GV)
+        h_evacuate(14, 2, 3, True)
+        h_evacuate(15, 0, 1, True)
+        y_scale(12)
+        y_round(12, YC_ENGINE)
+        h_evacuate(15, 1, 3, True)
+        h_quantize(14, 0, 2)
+        h_quantize(14, 2, 3)
+        average(14, 0, GV)
+        h_quantize(15, 0, 2)
+        h_quantize(15, 2, 3)
+        average(15, 0, GV)
+        bank3 = new_t_bank()
+        y_transpose(11, bank3, 0)
+        y_transpose(12, bank3, 1)
+        y_scale(13)
+        y_round(13, YC_TAIL)
+        y_quantize(10)
+        y_scale(14)
+        y_evacuate(11, True)
+        y_evacuate(12, True)
+        y_round(14, YC_TAIL)
+        bank4 = new_t_bank()
+        y_transpose(13, bank4, 0)
+        y_scale_round(15)
+        y_transpose(14, bank4, 1)
+        bank5 = new_t_bank()
+        y_transpose(15, bank5, 0)
+        y_scale(15)
+        y_evacuate(13, True)
+        y_evacuate(14, True)
+        y_evacuate(15, True)
+        y_quantize(11)
+        store_planes(8, 12)
+        store_scales(0, 12, [nc.sync])
+        y_quantize(12)
+        y_quantize(13)
+        y_quantize(14)
+        y_quantize(15)
+        store_planes(12, 16)
+        store_scales(12, 16, [nc.scalar, nc.sync])

@@ -22,17 +22,16 @@ TILES = G * PLANS // P
 TPP = PLANS // P
 GB = B // KP
 GV = V // KP
-
-X_LEAD = 2
-H_T_LAG = 2
-S2_LAG = 4
-Y_T_LAG = 5
 LAST = TILES - 1
-SPARE_FROM = 12
-YC_ENGINE = "gpsimd"
-YC_TAIL = "scalar"
-EVERY = 4
-LATE = 16
+NF = 2
+NW = 1
+D_BANKS = 3
+H_LAG = 1
+Y_LAG = 4
+X_STEPS = [4,5,6,7,8,9,10,11,12,13,14]
+B_STEPS = [14]
+YC_STEPS = [15]
+VSQ_STEPS = []
 
 
 def tile_fractionated_clonogen_survival_k7_kernel(
@@ -46,10 +45,9 @@ def tile_fractionated_clonogen_survival_k7_kernel(
 
     with ExitStack() as ctx:
         keep = ctx.enter_context(tc.tile_pool(name="keep", bufs=1))
-        work = ctx.enter_context(tc.tile_pool(name="work", bufs=5))
-        d_psum = ctx.enter_context(tc.psum_pool(name="d_psum", bufs=3))
-        t_psum = ctx.enter_context(tc.psum_pool(name="t_psum", bufs=4))
-        y_psum = ctx.enter_context(tc.psum_pool(name="y_psum", bufs=1))
+        work = ctx.enter_context(tc.tile_pool(name="work", bufs=3))
+        d_psum = ctx.enter_context(tc.psum_pool(name="d_psum", bufs=D_BANKS))
+        t_psum = ctx.enter_context(tc.psum_pool(name="t_psum", bufs=8 - D_BANKS))
         ctx.enter_context(tc.manual_schedule())
 
         x_sb = keep.tile([P, TILES, B], BF16, align_bytes=64)
@@ -57,7 +55,6 @@ def tile_fractionated_clonogen_survival_k7_kernel(
         a_scales = keep.tile([P, G * GB, V], U8, align_bytes=64)
         c_words = keep.tile([P, G * GV, 2 * O], U8, align_bytes=64)
         c_scales = keep.tile([P, G * GV, O], U8, align_bytes=64)
-        dens = keep.tile([P, G, V], BF16, align_bytes=64)
         burd = keep.tile([P, G * O], BF16, align_bytes=64)
         y_sb = keep.tile([P, TILES, O], F32, align_bytes=64)
         y_codes = keep.tile([P, TILES * P], U32, align_bytes=64)
@@ -66,7 +63,10 @@ def tile_fractionated_clonogen_survival_k7_kernel(
         reg_raw = keep.tile([TILES, P], BF16)
         reg_rows = keep.tile([P, P], F32)
         reg = keep.tile([P, TILES], F32)
+        dens_rows = keep.tile([P, KP], BF16)
+        dens = keep.tile([P, G * GV, 4], BF16)
         warm = keep.tile([P, 8], F32)
+        densb = keep.tile([P, G, NW * KP], BF16, align_bytes=64)
 
         def zero_plane(plane):
             nc.vector.memset(plane.rearrange("p g n -> p (g n)").bitcast(I32), 0)
@@ -88,8 +88,13 @@ def tile_fractionated_clonogen_survival_k7_kernel(
                 out=x_sb[:, i0:i1, :], in_=x_rows[i0 * P : i1 * P, :].rearrange("(i p) k -> p i k", p=P)
             )
 
-        def load_density(j):
-            nc.sync.dma_start(out=dens[:, j, :], in_=density[j].partition_broadcast(P))
+        def load_burden(j0, j1):
+            nc.sync.dma_start(
+                out=burd[:, j0 * O : j1 * O], in_=burden[j0:j1].rearrange("j o -> (j o)").partition_broadcast(P)
+            )
+
+        def load_density(j0, j1):
+            nc.sync.dma_start(out=densb[:, j0:j1, :], in_=density[j0:j1, NF * KP :].partition_broadcast(P))
 
         make_identity(nc, ident[:])
         zero_plane(a_scales[:, 0:GB, :])
@@ -98,43 +103,68 @@ def tile_fractionated_clonogen_survival_k7_kernel(
         load_x(0, 1)
         load_scales(a_scales, dose_scales, 0, GB)
         load_words(a_words, dose_words, 0, GB, slice(0, 2 * KP))
-        load_words(a_words, dose_words, 0, GB, slice(2 * KP, 2 * V))
         load_x(1, 2)
+        load_words(a_words, dose_words, 0, GB, slice(2 * KP, 2 * V))
+        nc.vector.memset(dens_rows[:].bitcast(I32), 0)
+        nc.vector.memset(reg_rows[:], 0.0)
         zero_plane(c_scales[:])
         zero_plane(a_scales[:, GB:, :])
-        nc.gpsimd.memset(reg_rows[:], 0.0)
-        load_density(0)
+        load_x(2, 4)
+        nc.sync.dma_start(out=dens_rows[0 : G * GV, :], in_=density.rearrange("j (g k) -> (j g) k", k=KP))
         nc.sync.dma_start(out=reg_raw[:], in_=regrowth.rearrange("j (m p) -> (j m) p", p=P))
-        load_x(2, TPP)
+        load_density(0, 1)
+        load_x(4, 5)
         load_scales(c_scales, member_scales, 0, G * GV)
         load_scales(a_scales, dose_scales, GB, G * GB)
         load_words(c_words, member_words, 0, GV)
-        nc.sync.dma_start(out=burd[:], in_=burden.rearrange("j o -> (j o)").partition_broadcast(P))
-        for j in range(1, G):
+        load_burden(0, 1)
+        load_x(5, 7)
+        load_words(a_words, dose_words, GB, 2 * GB)
+        load_x(7, 8)
+        load_density(1, G)
+        load_words(c_words, member_words, GV, 2 * GV)
+        load_burden(1, G)
+        for j in range(2, G):
             load_x(j * TPP, (j + 1) * TPP)
             load_words(a_words, dose_words, j * GB, (j + 1) * GB)
-            load_density(j)
             load_words(c_words, member_words, j * GV, (j + 1) * GV)
-        nc.gpsimd.tensor_copy(out=reg_rows[0:TILES, :], in_=reg_raw[:])
 
         def live(i):
             return 0 <= i < TILES
 
-        x_bank, x_grouped, x_q = {}, {}, {}
-        d_banks, squares, expo, h_bf, h_grouped, h_q = {}, {}, {}, {}, {}, {}
-        y_banks, y_bf = {}, {}
-        h_src, y_src, y_grouped = {}, {}, {}
+        x_bank, x_q, h_q = {}, {}, {}
+        d_banks, squares, expo, h_bank = {}, {}, {}, {}
+        y_banks, y_bf, y_src, y_grouped = {}, {}, {}, {}
+        staged, codes, h_bf, word_src, halves = {}, {}, {}, {}, []
 
         def new_t_bank():
             return t_psum.tile([P, KP], F32, name="t_bank")
 
-        def evacuate(on_scalar, dst_words, bank):
-            src = bank.rearrange("p (a u c) -> p a c u", u=2, c=P)
-            dst = dst_words.rearrange("p (a c u) -> p a c u", u=2, c=P)
-            if on_scalar:
+        def copy_on(engine, dst, src):
+            if engine == "scalar":
                 nc.scalar.copy(out=dst, in_=src)
             else:
                 nc.vector.tensor_copy(out=dst, in_=src)
+
+        def evacuate(engine, dst_words, bank):
+            src = bank.rearrange("p (a u c) -> p a c u", u=2, c=P)
+            copy_on(engine, dst_words.rearrange("p (a c u) -> p a c u", u=2, c=P), src)
+
+        def stage(key):
+            if key not in staged:
+                staged[key] = work.tile([P, B + V + O], BF16, align_bytes=64, name="staged", bufs=4)
+                qc = work.tile([P, (GB + GV) * P], U32, align_bytes=64, name="qc", bufs=4)
+                qs = work.tile([P, (GB + GV) * P], U8, align_bytes=64, name="qs", bufs=4)
+                codes[key] = (qc, qs)
+            return staged[key]
+
+        def quantize(key, g0, g1):
+            qc, qs = codes[key]
+            nc.vector.quantize_mx(
+                out=qc[:, g0 * P : g1 * P].bitcast(FP8X4),
+                scales=qs[:, g0 * P : g1 * P],
+                in_=staged[key][:, g0 * KP : g1 * KP],
+            )
 
         def x_transpose(i):
             x_bank[i] = new_t_bank()
@@ -146,98 +176,136 @@ def tile_fractionated_clonogen_survival_k7_kernel(
                         x_bank[i][:, c0 : c0 + P], words[:, 256 * g + u : 256 * (g + 1) : 2], ident[:]
                     )
 
-        def x_evacuate(i, on_scalar):
-            x_grouped[i] = work.tile([P, B], BF16, align_bytes=64, name="xg", bufs=3)
-            evacuate(on_scalar, x_grouped[i][:].bitcast(F32), x_bank[i][:])
-
-        def x_quantize(i):
-            xc = work.tile([P, GB * P], U32, align_bytes=64, name="xc")
-            xs = work.tile([P, GB * P], U8, align_bytes=64, name="xs")
-            x_q[i] = (xc, xs)
-            nc.vector.quantize_mx(out=xc[:].bitcast(FP8X4), scales=xs[:], in_=x_grouped[i][:])
+        def x_evacuate(i, key, engine):
+            x_q[i] = key
+            evacuate(engine, stage(key)[:, 0:B].bitcast(F32), x_bank[i][:])
 
         def dose(i, vg):
             j = i // TPP
-            xc, xs = x_q[i]
+            qc, qs = codes[x_q[i]]
             d_banks[i, vg] = d_psum.tile([P, KP], F32, name="d_bank")
             for g in range(GB):
                 nc.tensor.matmul_mx(
                     out=d_banks[i, vg][:],
-                    lhsT=xc[:, g * P : (g + 1) * P].bitcast(FP8X4),
-                    lhsT_scale=xs[:, g * P : (g + 1) * P],
+                    lhsT=qc[:, g * P : (g + 1) * P].bitcast(FP8X4),
+                    lhsT_scale=qs[:, g * P : (g + 1) * P],
                     rhs=a_words[:, j * GB + g, vg * 2 * KP : (vg + 1) * 2 * KP].bitcast(FP4X4),
                     rhs_scale=a_scales[:, j * GB + g, vg * KP : (vg + 1) * KP],
                     start=(g == 0),
                     stop=(g == GB - 1),
                 )
 
+        def word_part(tile, v0, v1, first=NF * KP):
+            return tile[:, first:].rearrange("q (u c) -> q u c", u=2)[:, :, (v0 - NF) * 256 : (v1 - NF) * 256]
+
         def square(i, vg):
             if vg == 0:
-                squares[i] = work.tile([P, 2, GV, 256], F32, name="sq", bufs=2)
-            nc.scalar.activation(
-                out=squares[i][:, :, vg, :].rearrange("q u (w e) -> q u w e", e=2),
-                in_=d_banks[i, vg][:].rearrange("q (w u e) -> q u w e", u=2, e=2),
-                func=ACT.Square,
-                bias=2.5,
+                squares[i] = work.tile([P, V], F32, name="sq", bufs=2)
+            if vg < NF:
+                dst = squares[i][:, vg * KP : (vg + 1) * KP].rearrange("q (t p) -> q t p", t=4)
+                src = d_banks[i, vg][:].rearrange("q (p t) -> q t p", t=4)
+            else:
+                dst = word_part(squares[i], vg, vg + 1).rearrange("q u (w e) -> q u w e", e=2)
+                src = d_banks[i, vg][:].rearrange("q (w u e) -> q u w e", u=2, e=2)
+            nc.scalar.activation(out=dst, in_=src, func=ACT.Square, bias=2.5)
+
+        def vector_square(i, vg):
+            shifted = work.tile([P, KP], F32, name="shifted", bufs=1)
+            nc.vector.tensor_scalar(
+                out=shifted[:].rearrange("q (t p) -> q t p", t=4),
+                in0=d_banks[i, vg][:].rearrange("q (p t) -> q t p", t=4),
+                scalar1=2.5,
+                scalar2=None,
+                op0=ALU.add,
+            )
+            nc.vector.tensor_tensor(
+                out=squares[i][:, vg * KP : (vg + 1) * KP], in0=shifted[:], in1=shifted[:], op=ALU.mult
             )
 
         def exponential(i, v0, v1):
             if v0 == 0:
-                expo[i] = work.tile([P, 2, GV, 256], F32, name="ex", bufs=3)
-            nc.scalar.activation(
-                out=expo[i][:, :, v0:v1, :], in_=squares[i][:, :, v0:v1, :], func=ACT.Exp, bias=0.9375, scale=-0.15
-            )
+                expo[i] = work.tile([P, V], F32, name="ex", bufs=3)
+            if v1 <= NF or v1 == GV and v0 <= NF:
+                dst, src = expo[i][:, v0 * KP : v1 * KP], squares[i][:, v0 * KP : v1 * KP]
+            else:
+                dst, src = word_part(expo[i], v0, v1), word_part(squares[i], v0, v1)
+            nc.scalar.activation(out=dst, in_=src, func=ACT.Exp, bias=0.9375, scale=-0.15)
 
         def times_density(i, v0, v1):
-            if v0 == 0:
-                h_bf[i] = work.tile([P, 2, GV, 256], BF16, align_bytes=64, name="hb", bufs=4)
+            if v0 == NF:
+                h_bf[i] = work.tile([P, NW * KP], BF16, align_bytes=64, name="hb")
             nc.vector.tensor_tensor(
-                out=h_bf[i][:, :, v0:v1, :].rearrange("q u g (w e) -> q u (g w) e", e=2),
-                in0=expo[i][:, :, v0:v1, :].rearrange("q u g (w e) -> q u (g w) e", e=2),
-                in1=dens[:, i // TPP, v0 * KP : v1 * KP].rearrange("q (w u e) -> q u w e", u=2, e=2),
+                out=word_part(h_bf[i], v0, v1, 0).rearrange("q u (w e) -> q u w e", e=2),
+                in0=word_part(expo[i], v0, v1).rearrange("q u (w e) -> q u w e", e=2),
+                in1=densb[:, i // TPP, (v0 - NF) * KP : (v1 - NF) * KP].rearrange("q (w u e) -> q u w e", u=2, e=2),
                 op=ALU.mult,
             )
 
-        def h_transpose(i, vg, bank, slot):
-            h_src[i, vg] = (bank, slot)
+        def half_bank():
+            if not halves:
+                bank = new_t_bank()
+                halves.extend([(bank, 1), (bank, 0)])
+            return halves.pop()
+
+        def word_transpose(name, words):
+            bank, slot = half_bank()
+            word_src[name] = (bank, slot)
             for u in range(2):
                 c0 = (2 * slot + u) * P
-                nc.tensor.transpose(bank[:, c0 : c0 + P], h_bf[i][:, u, vg, :].bitcast(F32), ident[:])
+                nc.tensor.transpose(bank[:, c0 : c0 + P], words[:, u, :], ident[:])
 
-        def y_transpose(i, bank, slot):
-            y_src[i] = (bank, slot)
-            for u in range(2):
-                c0 = (2 * slot + u) * P
-                nc.tensor.transpose(bank[:, c0 : c0 + P], y_bf[i][:, u, :].bitcast(F32), ident[:])
+        def hw_transpose(i, vg):
+            word_transpose(("h", i, vg), word_part(h_bf[i], vg, vg + 1, 0).bitcast(F32))
 
-        def new_grouped():
-            return work.tile([P, V + O], BF16, align_bytes=64, name="hg")
+        def yw_transpose(i):
+            word_transpose(("y", i), y_bf[i][:].bitcast(F32))
 
-        def h_quantize(i, v0, v1):
-            if v0 == 0:
-                hc = work.tile([P, GV * P], U32, align_bytes=64, name="hc")
-                hs = work.tile([P, GV * P], U8, align_bytes=64, name="hs")
-                h_q[i] = (hc, hs)
-            hc, hs = h_q[i]
+        def word_evacuate(name, n, key, col, engine):
+            bank, slot = word_src[name]
+            evacuate(
+                engine, stage(key)[:, col : col + n * KP].bitcast(F32), bank[:, slot * 256 : (slot + n) * 256]
+            )
+
+        def hw_evacuate(i, vg, n, key, engine):
+            h_q[i] = key
+            word_evacuate(("h", i, vg), n, key, B + vg * KP, engine)
+
+        def yw_evacuate(i, key, engine):
+            word_evacuate(("y", i), 1, key, B + V, engine)
+
+        def yw_quantize(i, key):
+            cols = slice(i * P, (i + 1) * P)
             nc.vector.quantize_mx(
-                out=hc[:, v0 * P : v1 * P].bitcast(FP8X4),
-                scales=hs[:, v0 * P : v1 * P],
-                in_=h_grouped[i][:, v0 * KP : v1 * KP],
+                out=y_codes[:, cols].bitcast(FP8X4), scales=y_scales[:, cols], in_=staged[key][:, B + V :]
+            )
+
+        def h_transpose(i, vg):
+            h_bank[i, vg] = new_t_bank()
+            for t in range(4):
+                c0 = vg * KP + t * P
+                nc.tensor.transpose(h_bank[i, vg][:, t * P : (t + 1) * P], expo[i][:, c0 : c0 + P], ident[:])
+
+        def h_evacuate(i, vg, key):
+            h_q[i] = key
+            k = (i // TPP) * GV + vg
+            nc.vector.tensor_tensor(
+                out=stage(key)[:, B + vg * KP : B + (vg + 1) * KP].rearrange("p (c t) -> p c t", t=4),
+                in0=h_bank[i, vg][:].rearrange("p (t c) -> p c t", t=4),
+                in1=dens[:, k : k + 1, :].to_broadcast([P, P, 4]),
+                op=ALU.mult,
             )
 
         def average(i, v0, v1):
             j = i // TPP
-            hc, hs = h_q[i]
+            qc, qs = codes[h_q[i]]
             if v0 == 0:
-                if i >= SPARE_FROM:
-                    y_banks[i] = d_psum.tile([P, O], F32, name="d_bank")
-                else:
-                    y_banks[i] = y_psum.tile([P, O], F32, name="y_bank")
+                y_banks[i] = d_psum.tile([P, O], F32, name="d_bank")
             for vg in range(v0, v1):
+                cols = slice((GB + vg) * P, (GB + vg + 1) * P)
                 nc.tensor.matmul_mx(
                     out=y_banks[i][:],
-                    lhsT=hc[:, vg * P : (vg + 1) * P].bitcast(FP8X4),
-                    lhsT_scale=hs[:, vg * P : (vg + 1) * P],
+                    lhsT=qc[:, cols].bitcast(FP8X4),
+                    lhsT_scale=qs[:, cols],
                     rhs=c_words[:, j * GV + vg, :].bitcast(FP4X4),
                     rhs_scale=c_scales[:, j * GV + vg, :],
                     start=(vg == 0),
@@ -257,42 +325,31 @@ def tile_fractionated_clonogen_survival_k7_kernel(
             nc.sync.dma_start(out=y_rows[i * P : (i + 1) * P, :], in_=y_sb[:, i, :])
 
         def y_round(i, engine):
-            y_bf[i] = work.tile([P, 2, 256], BF16, align_bytes=64, name="yb")
-            dst = y_bf[i][:].rearrange("q u (w e) -> q u w e", e=2)
-            src = y_sb[:, i, :].rearrange("q (w u e) -> q u w e", u=2, e=2)
-            if engine == "gpsimd":
-                nc.gpsimd.tensor_scalar(out=dst, in0=src, scalar1=1.0, scalar2=1.0, op0=ALU.mult, op1=ALU.mult)
-            elif engine == "scalar":
-                nc.scalar.copy(out=dst, in_=src)
-            else:
-                nc.vector.tensor_copy(out=dst, in_=src)
-
-        def y_scale_round(i):
-            j = i // TPP
-            y_bf[i] = work.tile([P, 2, 256], BF16, align_bytes=64, name="yb")
-            for u in range(2):
-                nc.vector.scalar_tensor_tensor(
-                    out=y_bf[i][:, u, :].rearrange("q (w e) -> q w e", e=2),
-                    in0=y_banks[i][:].rearrange("q (w u e) -> q u w e", u=2, e=2)[:, u],
-                    scalar=reg[:, i : i + 1],
-                    in1=burd[:, j * O : (j + 1) * O].rearrange("q (w u e) -> q u w e", u=2, e=2)[:, u],
-                    op0=ALU.mult,
-                    op1=ALU.mult,
-                )
-
-        def h_evacuate(i, v0, v1, on_scalar):
-            if i not in h_grouped:
-                h_grouped[i] = work.tile([P, V + O], BF16, align_bytes=64, name="hg")
-            bank, slot = h_src[i, v0]
-            n = (v1 - v0) * 256
-            evacuate(
-                on_scalar, h_grouped[i][:].bitcast(F32)[:, v0 * 256 : v1 * 256], bank[:, slot * 256 : slot * 256 + n]
+            y_bf[i] = work.tile([P, 2, 256], BF16, align_bytes=64, name="yb", bufs=4)
+            copy_on(
+                engine,
+                y_bf[i][:].rearrange("q u (w e) -> q u w e", e=2),
+                y_sb[:, i, :].rearrange("q (w u e) -> q u w e", u=2, e=2),
             )
 
-        def y_evacuate(i, on_scalar):
-            y_grouped[i] = work.tile([P, V + O], BF16, align_bytes=64, name="hg")
-            bank, slot = y_src[i]
-            evacuate(on_scalar, y_grouped[i][:].bitcast(F32)[:, 768:1024], bank[:, slot * 256 : slot * 256 + 256])
+        def y_transpose(i0, i1):
+            bank = new_t_bank()
+            y_src[i0] = bank
+            for i in range(i0, i1):
+                for u in range(2):
+                    c0 = (2 * (i - i0) + u) * P
+                    nc.tensor.transpose(bank[:, c0 : c0 + P], y_bf[i][:, u, :].bitcast(F32), ident[:])
+
+        def y_evacuate(i0, i1, engine):
+            y_grouped[i0] = work.tile([P, 2 * O], BF16, align_bytes=64, name="yg")
+            n = (i1 - i0) * 256
+            evacuate(engine, y_grouped[i0][:].bitcast(F32)[:, 0:n], y_src[i0][:, 0:n])
+
+        def y_quantize(i0, i1):
+            cols = slice(i0 * P, i1 * P)
+            nc.vector.quantize_mx(
+                out=y_codes[:, cols].bitcast(FP8X4), scales=y_scales[:, cols], in_=y_grouped[i0][:, 0 : (i1 - i0) * O]
+            )
 
         def store_planes(i0, i1):
             cols = slice(i0 * P, i1 * P)
@@ -305,144 +362,124 @@ def tile_fractionated_clonogen_survival_k7_kernel(
                     in_=y_scales[32 * q : 32 * q + 4, i0 * P : i1 * P].bitcast(I32),
                 )
 
-        def y_quantize(i):
-            cols = slice(i * P, (i + 1) * P)
-            nc.vector.quantize_mx(
-                out=y_codes[:, cols].bitcast(FP8X4), scales=y_scales[:, cols], in_=y_grouped[i][:, V : V + O]
+        def small_transposes():
+            bank = new_t_bank()
+            words = dens_rows[:].bitcast(F32)
+            for u in range(2):
+                nc.tensor.transpose(bank[:, u * P : (u + 1) * P], words[:, u : 256 : 2], ident[:])
+            nc.tensor.transpose(bank[:, 2 * P : 3 * P], reg_rows[:], ident[:])
+            return bank
+
+        def small_evacuate(bank):
+            nc.vector.tensor_copy(
+                out=dens[:].rearrange("p k t -> p (k t)").bitcast(F32).rearrange("p (k u) -> p k u", u=2),
+                in_=bank[:, 0 : 2 * P].rearrange("p (u c) -> p c u", u=2)[:, 0 : G * GV, :],
             )
+            nc.vector.tensor_copy(out=reg[:], in_=bank[:, 2 * P : 2 * P + TILES])
 
         x_transpose(0)
-        x_evacuate(0, False)
-        x_quantize(0)
-        a_bank, b_bank = {}, {}
-        reg_bank = None
-        for s in range(0, TILES):
-            ix, ih, iy = s - 1 + X_LEAD, s - 1 - H_T_LAG, s - 1 - Y_T_LAG
-            i2 = s - S2_LAG
-            late = s >= LATE
-            if live(ih):
-                hg = new_grouped()
-                h_grouped[ih] = hg
-                y_grouped[iy] = hg
-                words = hg[:].bitcast(F32)
-                if not late:
-                    evacuate(True, words[:, 0:512], a_bank[s - 1][:])
-                hi = 512 if live(iy) else 256
-                b_on_scalar = s % EVERY == 0 and not late
-                if b_on_scalar:
-                    evacuate(True, words[:, 512 : 512 + hi], b_bank[s - 1][:, 0:hi])
-            for vg in range(GV):
-                dose(s, vg)
-                if s == 0 and vg == 0:
-                    x_transpose(1)
-                square(s, vg)
-                if s == LAST and vg > 0:
-                    exponential(s, vg - 1, vg)
-            if live(i2 - 1):
-                y_scale(i2 - 1)
-                y_round(i2 - 1, YC_ENGINE)
+        x_evacuate(0, -1, "vector")
+        quantize(-1, 0, GB)
+        for s in range(TILES):
+            ix, ih, i2, iy = s + 1, s - 1 - H_LAG, s - 2 - H_LAG, s - 1 - Y_LAG
+            fine = s in (0, LAST)
+            dose(s, 0)
+            if s == 0:
+                x_transpose(1)
+                nc.vector.tensor_copy(out=reg_rows[0:TILES, :], in_=reg_raw[:])
+            if live(ih) and NF == 0:
+                hw_evacuate(ih, 0, 2, s, "scalar")
+            square(s, 0)
+            dose(s, 1)
+            if s in VSQ_STEPS:
+                vector_square(s, 1)
+            else:
+                square(s, 1)
+            if fine:
+                exponential(s, 0, 1)
             if live(i2):
                 average(i2, 0, GV)
-            if live(ix):
-                x_evacuate(ix, False)
             if s == 1:
-                nc.vector.tensor_copy(out=reg[:], in_=reg_bank[:, 0:TILES])
-            if live(ih):
-                if not b_on_scalar:
-                    evacuate(False, words[:, 512 : 512 + hi], b_bank[s - 1][:, 0:hi])
-                if late:
-                    evacuate(False, words[:, 0:512], a_bank[s - 1][:])
-            if s == LAST:
-                exponential(s, GV - 1, GV)
-            else:
-                exponential(s, 0, 2)
-                exponential(s, 2, 3)
+                small_evacuate(small_bank)
+            x_eng = "scalar" if s in X_STEPS else "vector"
+            b_eng = "scalar" if s in B_STEPS else "vector"
             if live(ix):
-                x_quantize(ix)
+                x_evacuate(ix, s, x_eng)
+            if live(ih):
+                for vg in range(NF):
+                    h_evacuate(ih, vg, s)
+                hw_evacuate(ih, 2, 2 if live(iy) else 1, s, b_eng)
+            dose(s, 2)
+            square(s, 2)
+            if fine:
+                exponential(s, 1, 2)
+                exponential(s, 2, 3)
+            else:
+                exponential(s, 0, GV)
             if live(s - 1):
-                times_density(s - 1, 0, GV)
+                times_density(s - 1, NF, GV)
+            if live(i2):
+                y_scale(i2)
+            if live(ix) and live(ih):
+                quantize(s, 0, 4)
+                quantize(s, 4, 5)
+            elif live(ix):
+                quantize(s, 0, 2)
+            else:
+                quantize(s, 2, 4)
+                quantize(s, 4, 5)
+            if live(i2):
+                y_round(i2, "scalar" if s in YC_STEPS else "vector")
             if live(iy):
-                y_quantize(iy)
+                yw_quantize(iy, s)
                 if iy % TPP == TPP - 1:
                     store_planes(iy + 1 - TPP, iy + 1)
-            if live(ih):
-                h_quantize(ih, 0, 2)
-                h_quantize(ih, 2, 3)
-
-            tx, th, ty = s + X_LEAD, s - H_T_LAG, s - Y_T_LAG
-            if live(tx):
-                x_transpose(tx)
+            if live(s + 2):
+                x_transpose(s + 2)
             if s == 0:
-                reg_bank = new_t_bank()
-                nc.tensor.transpose(reg_bank[:, 0:P], reg_rows[:], ident[:])
+                small_bank = small_transposes()
+            th, ty = s - H_LAG, s - Y_LAG
             if live(th):
-                a_bank[s] = new_t_bank()
-                b_bank[s] = new_t_bank()
-            if live(ty):
-                y_transpose(ty, b_bank[s], 1)
-            if live(th):
-                for vg in range(GV):
-                    h_transpose(th, vg, a_bank[s] if vg < 2 else b_bank[s], vg % 2)
-
-        times_density(15, 0, 1)
-        average(12, 0, GV)
-        bank0, bank1 = new_t_bank(), None
-        h_transpose(14, 0, bank0, 0)
-        h_transpose(14, 1, bank0, 1)
-        y_scale(11)
-        y_round(11, YC_ENGINE)
-        h_evacuate(13, 0, 2, True)
-        times_density(15, 1, 2)
-        h_evacuate(13, 2, 3, True)
-        bank1 = new_t_bank()
-        h_transpose(14, 2, bank1, 0)
-        h_transpose(15, 0, bank1, 1)
-        y_evacuate(10, True)
-        times_density(15, 2, 3)
-        h_evacuate(14, 0, 2, True)
-        bank2 = new_t_bank()
-        h_transpose(15, 1, bank2, 0)
-        h_transpose(15, 2, bank2, 1)
-        h_quantize(13, 0, 2)
-        h_quantize(13, 2, 3)
+                for vg in range(NF):
+                    h_transpose(th, vg)
+                for vg in range(NF, GV):
+                    hw_transpose(th, vg)
+                if live(ty):
+                    yw_transpose(ty)
+                halves.clear()
+        h_transpose(15, 0)
         average(13, 0, GV)
-        h_evacuate(14, 2, 3, True)
-        h_evacuate(15, 0, 1, True)
-        y_scale(12)
-        y_round(12, YC_ENGINE)
-        h_evacuate(15, 1, 3, True)
-        h_quantize(14, 0, 2)
-        h_quantize(14, 2, 3)
-        average(14, 0, GV)
-        h_quantize(15, 0, 2)
-        h_quantize(15, 2, 3)
-        average(15, 0, GV)
-        bank3 = new_t_bank()
-        y_transpose(11, bank3, 0)
-        y_transpose(12, bank3, 1)
+        h_evacuate(14, 0, 16)
+        h_evacuate(14, 1, 16)
+        h_evacuate(15, 0, 17)
+        times_density(15, 2, 3)
+        quantize(16, 2, 4)
+        hw_evacuate(14, 2, 2, 16, "scalar")
+        h_transpose(15, 1)
+        h_evacuate(15, 1, 17)
+        hw_transpose(15, 2)
+        yw_transpose(12)
+        hw_evacuate(15, 2, 2, 17, "scalar")
+        quantize(16, 4, 5)
+        quantize(17, 2, 4)
         y_scale(13)
-        y_round(13, YC_TAIL)
-        y_quantize(10)
+        average(14, 0, GV)
+        quantize(17, 4, 5)
         y_scale(14)
-        y_evacuate(11, True)
-        y_evacuate(12, True)
-        y_round(14, YC_TAIL)
-        bank4 = new_t_bank()
-        y_transpose(13, bank4, 0)
-        y_scale_round(15)
-        y_transpose(14, bank4, 1)
-        bank5 = new_t_bank()
-        y_transpose(15, bank5, 0)
-        y_scale(15)
-        y_evacuate(13, True)
-        y_evacuate(14, True)
-        y_evacuate(15, True)
-        y_quantize(11)
-        store_planes(8, 12)
+        y_round(13, "scalar")
+        y_round(14, "scalar")
+        average(15, 0, GV)
+        yw_quantize(11, 16)
         store_scales(0, 12, [nc.sync])
-        y_quantize(12)
-        y_quantize(13)
-        y_quantize(14)
-        y_quantize(15)
+        y_scale(15)
+        y_transpose(13, 15)
+        yw_quantize(12, 17)
+        y_round(15, "vector")
+        y_evacuate(13, 15, "vector")
+        y_quantize(13, 15)
+        y_transpose(15, 16)
+        y_evacuate(15, 16, "scalar")
+        store_planes(8, 12)
+        y_quantize(15, 16)
         store_planes(12, 16)
         store_scales(12, 16, [nc.scalar, nc.sync])

@@ -23,12 +23,20 @@ TPP = PLANS // P
 GB = B // KP
 GV = V // KP
 LAST = TILES - 1
+YC_FROM = 11
+SPLIT = 1
+WE_FROM = 16
+DX = 3
+DY = 4
+X_FROM = 7
+EVERY = 3
+YC = "vector"
 NF = 2
 NW = 1
-D_BANKS = 3
+D_BANKS = 4
 H_LAG = 1
 Y_LAG = 4
-X_STEPS = [4,5,6,7,8,9,10,11,12,13,14]
+X_STEPS = [4, 5, 6, 7, 8, 9, 10, 11, 12, 13, 14]
 B_STEPS = [14]
 YC_STEPS = [15]
 VSQ_STEPS = []
@@ -96,38 +104,42 @@ def tile_fractionated_clonogen_survival_k7_kernel(
         def load_density(j0, j1):
             nc.sync.dma_start(out=densb[:, j0:j1, :], in_=density[j0:j1, NF * KP :].partition_broadcast(P))
 
-        make_identity(nc, ident[:])
         zero_plane(a_scales[:, 0:GB, :])
+        make_identity(nc, ident[:])
         nc.vector.memset(warm[:], 0.0)
         nc.scalar.activation(out=warm[:, 4:5], in_=warm[:, 0:1], func=ACT.Exp)
-        load_x(0, 1)
-        load_scales(a_scales, dose_scales, 0, GB)
+        for g in range(GB):
+            nc.sync.dma_start(out=x_sb[:, 0, g * KP : (g + 1) * KP], in_=x_rows[0:P, g * KP : (g + 1) * KP])
         load_words(a_words, dose_words, 0, GB, slice(0, 2 * KP))
+        load_scales(a_scales, dose_scales, 0, GB)
         load_x(1, 2)
         load_words(a_words, dose_words, 0, GB, slice(2 * KP, 2 * V))
         nc.vector.memset(dens_rows[:].bitcast(I32), 0)
         nc.vector.memset(reg_rows[:], 0.0)
-        zero_plane(c_scales[:])
-        zero_plane(a_scales[:, GB:, :])
         load_x(2, 4)
         nc.sync.dma_start(out=dens_rows[0 : G * GV, :], in_=density.rearrange("j (g k) -> (j g) k", k=KP))
         nc.sync.dma_start(out=reg_raw[:], in_=regrowth.rearrange("j (m p) -> (j m) p", p=P))
+        nc.gpsimd.tensor_copy(out=reg_rows[0:TILES, :], in_=reg_raw[:])
         load_density(0, 1)
         load_x(4, 5)
-        load_scales(c_scales, member_scales, 0, G * GV)
-        load_scales(a_scales, dose_scales, GB, G * GB)
-        load_words(c_words, member_words, 0, GV)
-        load_burden(0, 1)
-        load_x(5, 7)
-        load_words(a_words, dose_words, GB, 2 * GB)
-        load_x(7, 8)
-        load_density(1, G)
-        load_words(c_words, member_words, GV, 2 * GV)
-        load_burden(1, G)
-        for j in range(2, G):
-            load_x(j * TPP, (j + 1) * TPP)
-            load_words(a_words, dose_words, j * GB, (j + 1) * GB)
-            load_words(c_words, member_words, j * GV, (j + 1) * GV)
+
+        def later_loads():
+            zero_plane(c_scales[:])
+            zero_plane(a_scales[:, GB:, :])
+            load_scales(c_scales, member_scales, 0, G * GV)
+            load_scales(a_scales, dose_scales, GB, G * GB)
+            load_words(c_words, member_words, 0, GV)
+            load_burden(0, 1)
+            load_x(5, 7)
+            load_words(a_words, dose_words, GB, 2 * GB)
+            load_x(7, 8)
+            load_density(1, G)
+            load_words(c_words, member_words, GV, 2 * GV)
+            load_burden(1, G)
+            for j in range(2, G):
+                load_x(j * TPP, (j + 1) * TPP)
+                load_words(a_words, dose_words, j * GB, (j + 1) * GB)
+                load_words(c_words, member_words, j * GV, (j + 1) * GV)
 
         def live(i):
             return 0 <= i < TILES
@@ -143,6 +155,8 @@ def tile_fractionated_clonogen_survival_k7_kernel(
         def copy_on(engine, dst, src):
             if engine == "scalar":
                 nc.scalar.copy(out=dst, in_=src)
+            elif engine == "gpsimd":
+                nc.gpsimd.tensor_scalar(out=dst, in0=src, scalar1=1.0, scalar2=1.0, op0=ALU.mult, op1=ALU.mult)
             else:
                 nc.vector.tensor_copy(out=dst, in_=src)
 
@@ -332,6 +346,27 @@ def tile_fractionated_clonogen_survival_k7_kernel(
                 y_sb[:, i, :].rearrange("q (w u e) -> q u w e", u=2, e=2),
             )
 
+        def y_scale_round(i):
+            j = i // TPP
+            y_bf[i] = work.tile([P, 2, 256], BF16, align_bytes=64, name="yb", bufs=4)
+            for u in range(2):
+                nc.vector.scalar_tensor_tensor(
+                    out=y_bf[i][:, u, :].rearrange("q (w e) -> q w e", e=2),
+                    in0=y_banks[i][:].rearrange("q (w u e) -> q u w e", u=2, e=2)[:, u],
+                    scalar=reg[:, i : i + 1],
+                    in1=burd[:, j * O : (j + 1) * O].rearrange("q (w u e) -> q u w e", u=2, e=2)[:, u],
+                    op0=ALU.mult,
+                    op1=ALU.mult,
+                )
+
+        def x_half(g, engine):
+            bank = new_t_bank()
+            words = x_sb[:, 0, :].bitcast(F32)
+            for u in range(2):
+                nc.tensor.transpose(bank[:, u * P : (u + 1) * P], words[:, 256 * g + u : 256 * (g + 1) : 2], ident[:])
+            x_q[0] = -DX
+            evacuate(engine, stage(-DX)[:, g * KP : (g + 1) * KP].bitcast(F32), bank[:, 0:256])
+
         def y_transpose(i0, i1):
             bank = new_t_bank()
             y_src[i0] = bank
@@ -377,109 +412,188 @@ def tile_fractionated_clonogen_survival_k7_kernel(
             )
             nc.vector.tensor_copy(out=reg[:], in_=bank[:, 2 * P : 2 * P + TILES])
 
-        x_transpose(0)
-        x_evacuate(0, -1, "vector")
-        quantize(-1, 0, GB)
-        for s in range(TILES):
-            ix, ih, i2, iy = s + 1, s - 1 - H_LAG, s - 2 - H_LAG, s - 1 - Y_LAG
-            fine = s in (0, LAST)
-            dose(s, 0)
-            if s == 0:
-                x_transpose(1)
-                nc.vector.tensor_copy(out=reg_rows[0:TILES, :], in_=reg_raw[:])
-            if live(ih) and NF == 0:
-                hw_evacuate(ih, 0, 2, s, "scalar")
-            square(s, 0)
-            dose(s, 1)
-            if s in VSQ_STEPS:
-                vector_square(s, 1)
-            else:
-                square(s, 1)
-            if fine:
-                exponential(s, 0, 1)
-            if live(i2):
-                average(i2, 0, GV)
-            if s == 1:
-                small_evacuate(small_bank)
-            x_eng = "scalar" if s in X_STEPS else "vector"
-            b_eng = "scalar" if s in B_STEPS else "vector"
-            if live(ix):
-                x_evacuate(ix, s, x_eng)
-            if live(ih):
-                for vg in range(NF):
-                    h_evacuate(ih, vg, s)
-                hw_evacuate(ih, 2, 2 if live(iy) else 1, s, b_eng)
-            dose(s, 2)
-            square(s, 2)
-            if fine:
-                exponential(s, 1, 2)
-                exponential(s, 2, 3)
-            else:
-                exponential(s, 0, GV)
-            if live(s - 1):
-                times_density(s - 1, NF, GV)
-            if live(i2):
-                y_scale(i2)
-            if live(ix) and live(ih):
-                quantize(s, 0, 4)
-                quantize(s, 4, 5)
-            elif live(ix):
-                quantize(s, 0, 2)
-            else:
-                quantize(s, 2, 4)
-                quantize(s, 4, 5)
-            if live(i2):
-                y_round(i2, "scalar" if s in YC_STEPS else "vector")
-            if live(iy):
-                yw_quantize(iy, s)
-                if iy % TPP == TPP - 1:
-                    store_planes(iy + 1 - TPP, iy + 1)
-            if live(s + 2):
-                x_transpose(s + 2)
-            if s == 0:
-                small_bank = small_transposes()
-            th, ty = s - H_LAG, s - Y_LAG
-            if live(th):
-                for vg in range(NF):
-                    h_transpose(th, vg)
-                for vg in range(NF, GV):
-                    hw_transpose(th, vg)
-                if live(ty):
-                    yw_transpose(ty)
-                halves.clear()
-        h_transpose(15, 0)
-        average(13, 0, GV)
-        h_evacuate(14, 0, 16)
-        h_evacuate(14, 1, 16)
-        h_evacuate(15, 0, 17)
-        times_density(15, 2, 3)
-        quantize(16, 2, 4)
-        hw_evacuate(14, 2, 2, 16, "scalar")
-        h_transpose(15, 1)
-        h_evacuate(15, 1, 17)
-        hw_transpose(15, 2)
-        yw_transpose(12)
-        hw_evacuate(15, 2, 2, 17, "scalar")
-        quantize(16, 4, 5)
-        quantize(17, 2, 4)
-        y_scale(13)
-        average(14, 0, GV)
-        quantize(17, 4, 5)
-        y_scale(14)
+        def st_xt(k):
+            if 0 < k + DX < TILES:
+                x_transpose(k + DX)
+
+        def st_xe(k, engine):
+            if 0 < k + DX < TILES:
+                x_evacuate(k + DX, k, engine if k + DX >= X_FROM else "vector")
+
+        def st_q1(k):
+            has_x, has_h = 0 < k + DX < TILES, live(k)
+            if has_x or has_h:
+                quantize(k, 0 if has_x else 2, 4 if has_h else 2)
+
+        def st_wt(k):
+            halves.clear()
+            if live(k):
+                hw_transpose(k, 2)
+            elif live(k - DY):
+                half_bank_skip()
+            if live(k - DY):
+                yw_transpose(k - DY)
+
+        def half_bank_skip():
+            half_bank()
+
+        def st_we(k, engine):
+            if k < 13 and (k % EVERY == 0 or k >= WE_FROM):
+                engine = "scalar"
+            if live(k):
+                hw_evacuate(k, 2, 2 if live(k - DY) else 1, k, engine)
+            elif live(k - DY):
+                yw_evacuate(k - DY, k, engine)
+
+        def st_yq(k):
+            i = k - DY
+            if live(i):
+                yw_quantize(i, k)
+                if i == LAST - 1:
+                    store_planes(LAST + 1 - TPP, LAST)
+                elif i == LAST:
+                    store_planes(LAST, TILES)
+                    store_scales(LAST + 1 - TPP, TILES, [nc.scalar, nc.sync])
+                elif i % TPP == TPP - 1:
+                    store_planes(i + 1 - TPP, i + 1)
+                if i == LAST - TPP:
+                    store_scales(0, i + 1, [nc.sync])
+
+        def st_ys(i):
+            if i == LAST:
+                y_scale_round(i)
+            y_scale(i)
+
+        def st_yc(i):
+            if i < LAST:
+                y_round(i, "scalar" if i >= YC_FROM else YC)
+
+        def st_ex(i, part):
+            if i == 0 or i == LAST or SPLIT:
+                exponential(i, 2 * part, 2 + part)
+            elif part == 1:
+                exponential(i, 0, 3)
+
+        def on(i, f, *args):
+            if live(i):
+                f(i, *args)
+
+        x_half(0, "vector")
+        quantize(-DX, 0, 1)
+        x_half(1, "vector")
+        st_xt(-2)
+        quantize(-DX, 1, 2)
+        on(0, dose, 0)
+        on(0, dose, 1)
+        x_evacuate(1, -2, "vector")
+        on(0, dose, 2)
+        on(0, square, 0)
+        st_q1(-2)
+        on(1, dose, 2)
+        st_xt(-1)
+        small_bank = small_transposes()
+        on(1, dose, 0)
+        later_loads()
+        x_evacuate(2, -1, "vector")
+        on(0, square, 1)
+        st_q1(-1)
+        on(0, square, 2)
+        on(1, dose, 1)
+        on(0, st_ex, 0)
+        on(0, st_ex, 1)
+        on(1, square, 0)
+        on(1, square, 1)
+        on(0, times_density, 2, 3)
+        st_xt(0)
+        small_evacuate(small_bank)
+        on(1, square, 2)
+        x_evacuate(3, 0, "vector")
+        on(0, h_transpose, 1)
+        on(1, st_ex, 0)
+        on(0, h_transpose, 0)
+        on(2, dose, 0)
+        on(2, dose, 1)
+        on(0, lambda i: h_evacuate(i, 1, i))
+        st_wt(0)
+        on(0, lambda i: h_evacuate(i, 0, i))
+        on(2, dose, 2)
+        on(1, st_ex, 1)
+        for s in range(3, 16):
+            on(s - 1, square, 0)
+            st_yq(s - 6)
+            st_we(s - 3, "vector")
+            on(s - 2, h_transpose, 0)
+            on(s - 2, times_density, 2, 3)
+            on(s - 1, square, 1)
+            st_xt(s - 2)
+            on(s - 2, h_transpose, 1)
+            st_q1(s - 3)
+            on(s - 5, st_yc)
+            on(s - 1, square, 2)
+            st_wt(s - 2)
+            on(s - 2, lambda i: h_evacuate(i, 0, i))
+            on(s - 1, st_ex, 0)
+            on(s - 0, dose, 0)
+            on(s - 4, st_ys)
+            on(s - 0, dose, 1)
+            on(s - 2, lambda i: h_evacuate(i, 1, i))
+            on(s - 0, dose, 2)
+            on(s - 3, quantize, 4, 5)
+            on(s - 3, average, 0, GV)
+            on(s - 1, st_ex, 1)
+            st_xe(s - 2, "scalar")
+        on(14, h_transpose, 1)
+        on(15, square, 0)
+        on(15, square, 1)
+        st_yq(10)
+        st_q1(13)
+        on(14, h_transpose, 0)
+        st_we(13, "vector")
+        on(14, times_density, 2, 3)
+        st_wt(14)
+        on(13, quantize, 4, 5)
+        on(15, square, 2)
+        on(14, lambda i: h_evacuate(i, 0, i))
+        on(15, st_ex, 0)
+        on(14, lambda i: h_evacuate(i, 1, i))
+        on(15, st_ex, 1)
+        st_we(14, "scalar")
+        on(15, h_transpose, 0)
+        on(15, h_transpose, 1)
+        on(12, st_ys)
+        st_yq(13)
+        st_q1(14)
+        y_round(11, "scalar")
+        st_yq(11)
+        on(13, average, 0, GV)
+        on(15, times_density, 2, 3)
+        st_wt(15)
+        on(14, quantize, 4, 5)
+        st_we(15, "scalar")
+        on(15, lambda i: h_evacuate(i, 0, i))
+        y_round(12, "scalar")
+        on(15, lambda i: h_evacuate(i, 1, i))
+        on(13, st_ys)
+        on(15, quantize, 4, 5)
+        on(14, average, 0, GV)
+        st_q1(15)
         y_round(13, "scalar")
+        on(14, st_ys)
+        st_wt(16)
+        st_yq(14)
+        on(15, average, 0, GV)
+        st_wt(17)
         y_round(14, "scalar")
-        average(15, 0, GV)
-        yw_quantize(11, 16)
-        store_scales(0, 12, [nc.sync])
-        y_scale(15)
-        y_transpose(13, 15)
-        yw_quantize(12, 17)
-        y_round(15, "vector")
-        y_evacuate(13, 15, "vector")
-        y_quantize(13, 15)
-        y_transpose(15, 16)
-        y_evacuate(15, 16, "scalar")
-        store_planes(8, 12)
-        y_quantize(15, 16)
-        store_planes(12, 16)
-        store_scales(12, 16, [nc.scalar, nc.sync])
+        st_yq(12)
+        st_yq(15)
+        st_we(17, "scalar")
+        on(15, st_ys)
+        st_we(16, "scalar")
+        st_wt(18)
+        st_wt(19)
+        st_yq(16)
+        st_we(18, "scalar")
+        st_we(19, "scalar")
+        st_yq(17)
+        st_yq(18)
+        st_yq(19)

@@ -23,13 +23,13 @@ TPP = PLANS // P
 GB = B // KP
 GV = V // KP
 LAST = TILES - 1
-YC_FROM = 11
+YC_FROM = 13
 SPLIT = 1
 WE_FROM = 16
 DX = 3
 DY = 4
 X_FROM = 7
-EVERY = 3
+EVERY = 2
 YC = "vector"
 NF = 2
 NW = 1
@@ -63,7 +63,6 @@ def tile_fractionated_clonogen_survival_k7_kernel(
         a_scales = keep.tile([P, G * GB, V], U8, align_bytes=64)
         c_words = keep.tile([P, G * GV, 2 * O], U8, align_bytes=64)
         c_scales = keep.tile([P, G * GV, O], U8, align_bytes=64)
-        burd = keep.tile([P, G * O], BF16, align_bytes=64)
         y_sb = keep.tile([P, TILES, O], F32, align_bytes=64)
         y_codes = keep.tile([P, TILES * P], U32, align_bytes=64)
         y_scales = keep.tile([P, TILES * P], U8, align_bytes=64)
@@ -74,7 +73,8 @@ def tile_fractionated_clonogen_survival_k7_kernel(
         dens_rows = keep.tile([P, KP], BF16)
         dens = keep.tile([P, G * GV, 4], BF16)
         warm = keep.tile([P, 8], F32)
-        densb = keep.tile([P, G, NW * KP], BF16, align_bytes=64)
+        spread = keep.tile([P, G, 2 * KP], BF16, align_bytes=64)
+        burd_words = keep.tile([P, 2 * G], F32)
 
         def zero_plane(plane):
             nc.vector.memset(plane.rearrange("p g n -> p (g n)").bitcast(I32), 0)
@@ -96,14 +96,6 @@ def tile_fractionated_clonogen_survival_k7_kernel(
                 out=x_sb[:, i0:i1, :], in_=x_rows[i0 * P : i1 * P, :].rearrange("(i p) k -> p i k", p=P)
             )
 
-        def load_burden(j0, j1):
-            nc.sync.dma_start(
-                out=burd[:, j0 * O : j1 * O], in_=burden[j0:j1].rearrange("j o -> (j o)").partition_broadcast(P)
-            )
-
-        def load_density(j0, j1):
-            nc.sync.dma_start(out=densb[:, j0:j1, :], in_=density[j0:j1, NF * KP :].partition_broadcast(P))
-
         zero_plane(a_scales[:, 0:GB, :])
         make_identity(nc, ident[:])
         nc.vector.memset(warm[:], 0.0)
@@ -119,23 +111,28 @@ def tile_fractionated_clonogen_survival_k7_kernel(
         load_x(2, 4)
         nc.sync.dma_start(out=dens_rows[0 : G * GV, :], in_=density.rearrange("j (g k) -> (j g) k", k=KP))
         nc.sync.dma_start(out=reg_raw[:], in_=regrowth.rearrange("j (m p) -> (j m) p", p=P))
+        nc.sync.dma_start(
+            out=reg_rows[32 : 32 + 2 * G, :], in_=burden.bitcast(F32).rearrange("j (m p) -> (j m) p", p=P)
+        )
         nc.gpsimd.tensor_copy(out=reg_rows[0:TILES, :], in_=reg_raw[:])
-        load_density(0, 1)
-        load_x(4, 5)
+        load_x(4, 6)
+
+        zeroed = {}
+
+        def zero_c():
+            zeroed["c"] = zero_plane(c_scales[:])
+
+        def zero_a(j):
+            zeroed[j] = zero_plane(a_scales[:, j * GB : (j + 1) * GB, :])
 
         def later_loads():
-            zero_plane(c_scales[:])
-            zero_plane(a_scales[:, GB:, :])
+            assert len(zeroed) == G
             load_scales(c_scales, member_scales, 0, G * GV)
             load_scales(a_scales, dose_scales, GB, G * GB)
             load_words(c_words, member_words, 0, GV)
-            load_burden(0, 1)
-            load_x(5, 7)
             load_words(a_words, dose_words, GB, 2 * GB)
-            load_x(7, 8)
-            load_density(1, G)
+            load_x(6, 8)
             load_words(c_words, member_words, GV, 2 * GV)
-            load_burden(1, G)
             for j in range(2, G):
                 load_x(j * TPP, (j + 1) * TPP)
                 load_words(a_words, dose_words, j * GB, (j + 1) * GB)
@@ -147,7 +144,7 @@ def tile_fractionated_clonogen_survival_k7_kernel(
         x_bank, x_q, h_q = {}, {}, {}
         d_banks, squares, expo, h_bank = {}, {}, {}, {}
         y_banks, y_bf, y_src, y_grouped = {}, {}, {}, {}
-        staged, codes, h_bf, word_src, halves = {}, {}, {}, {}, []
+        staged, codes, h_bf, word_src, halves, spread_bank = {}, {}, {}, {}, [], {}
 
         def new_t_bank():
             return t_psum.tile([P, KP], F32, name="t_bank")
@@ -251,7 +248,7 @@ def tile_fractionated_clonogen_survival_k7_kernel(
             nc.vector.tensor_tensor(
                 out=word_part(h_bf[i], v0, v1, 0).rearrange("q u (w e) -> q u w e", e=2),
                 in0=word_part(expo[i], v0, v1).rearrange("q u (w e) -> q u w e", e=2),
-                in1=densb[:, i // TPP, (v0 - NF) * KP : (v1 - NF) * KP].rearrange("q (w u e) -> q u w e", u=2, e=2),
+                in1=spread[:, i // TPP, 0:KP].rearrange("q (u w e) -> q u w e", u=2, e=2),
                 op=ALU.mult,
             )
 
@@ -332,7 +329,7 @@ def tile_fractionated_clonogen_survival_k7_kernel(
                 out=y_sb[:, i, :],
                 in0=y_banks[i][:],
                 scalar=reg[:, i : i + 1],
-                in1=burd[:, j * O : (j + 1) * O],
+                in1=spread[:, j, KP:],
                 op0=ALU.mult,
                 op1=ALU.mult,
             )
@@ -354,7 +351,7 @@ def tile_fractionated_clonogen_survival_k7_kernel(
                     out=y_bf[i][:, u, :].rearrange("q (w e) -> q w e", e=2),
                     in0=y_banks[i][:].rearrange("q (w u e) -> q u w e", u=2, e=2)[:, u],
                     scalar=reg[:, i : i + 1],
-                    in1=burd[:, j * O : (j + 1) * O].rearrange("q (w u e) -> q u w e", u=2, e=2)[:, u],
+                    in1=spread[:, j, KP:].rearrange("q (w u e) -> q u w e", u=2, e=2)[:, u],
                     op0=ALU.mult,
                     op1=ALU.mult,
                 )
@@ -411,6 +408,34 @@ def tile_fractionated_clonogen_survival_k7_kernel(
                 in_=bank[:, 0 : 2 * P].rearrange("p (u c) -> p c u", u=2)[:, 0 : G * GV, :],
             )
             nc.vector.tensor_copy(out=reg[:], in_=bank[:, 2 * P : 2 * P + TILES])
+            nc.vector.tensor_copy(out=burd_words[:], in_=bank[:, 2 * P + 32 : 2 * P + 32 + 2 * G])
+
+        def spread_transpose(j):
+            spread_bank[j] = d_psum.tile([P, KP], F32, name="d_bank")
+            dens_words = dens[:].rearrange("p k t -> p (k t)").bitcast(F32)
+            for u in range(2):
+                c = 2 * (j * GV + GV - 1) + u
+                nc.tensor.transpose(
+                    spread_bank[j][:, u * P : (u + 1) * P], dens_words[:, c : c + 1].to_broadcast([P, P]), ident[:]
+                )
+            for m in range(2):
+                c = 2 * j + m
+                nc.tensor.transpose(
+                    spread_bank[j][:, (2 + m) * P : (3 + m) * P],
+                    burd_words[:, c : c + 1].to_broadcast([P, P]),
+                    ident[:],
+                )
+
+        def spread_evacuate(j, engine):
+            copy_on(engine, spread[:, j, :].bitcast(F32), spread_bank[j][:])
+
+        def st_sp(s):
+            if s % TPP == 0 and 0 < s // TPP < G:
+                spread_transpose(s // TPP)
+
+        def st_se(s, engine):
+            if s % TPP == 0 and 0 < s // TPP < G:
+                spread_evacuate(s // TPP, engine)
 
         def st_xt(k):
             if 0 < k + DX < TILES:
@@ -479,121 +504,129 @@ def tile_fractionated_clonogen_survival_k7_kernel(
                 f(i, *args)
 
         x_half(0, "vector")
+        x_half(1, "scalar")
         quantize(-DX, 0, 1)
-        x_half(1, "vector")
-        st_xt(-2)
         quantize(-DX, 1, 2)
         on(0, dose, 0)
-        on(0, dose, 1)
-        x_evacuate(1, -2, "vector")
-        on(0, dose, 2)
-        on(0, square, 0)
-        st_q1(-2)
-        on(1, dose, 2)
-        st_xt(-1)
-        small_bank = small_transposes()
-        on(1, dose, 0)
+        st_xt(-2)
+        zero_a(1)
+        zero_c()
+        zero_a(2)
+        zero_a(3)
         later_loads()
-        x_evacuate(2, -1, "vector")
+        on(0, square, 0)
+        x_evacuate(1, -2, "scalar")
+        on(0, dose, 1)
         on(0, square, 1)
-        st_q1(-1)
-        on(0, square, 2)
-        on(1, dose, 1)
+        on(0, dose, 2)
+        small_bank = small_transposes()
+        st_xt(-1)
         on(0, st_ex, 0)
-        on(0, st_ex, 1)
-        on(1, square, 0)
-        on(1, square, 1)
-        on(0, times_density, 2, 3)
-        st_xt(0)
+        st_q1(-2)
+        on(1, dose, 0)
         small_evacuate(small_bank)
-        on(1, square, 2)
-        x_evacuate(3, 0, "vector")
-        on(0, h_transpose, 1)
-        on(1, st_ex, 0)
-        on(0, h_transpose, 0)
-        on(2, dose, 0)
+        x_evacuate(2, -1, "vector")
+        on(0, square, 2)
+        spread_transpose(0)
+        on(1, square, 0)
+        st_q1(-1)
+        on(1, dose, 1)
+        on(1, dose, 2)
+        on(0, st_ex, 1)
+        spread_evacuate(0, "vector")
+        on(1, square, 1)
         on(2, dose, 1)
-        on(0, lambda i: h_evacuate(i, 1, i))
+        on(0, h_transpose, 1)
+        on(1, square, 2)
+        on(0, h_transpose, 0)
+        on(0, times_density, 2, 3)
+        on(1, st_ex, 0)
+        on(1, st_ex, 1)
+        st_xt(0)
         st_wt(0)
+        on(2, dose, 0)
+        on(0, lambda i: h_evacuate(i, 1, i))
         on(0, lambda i: h_evacuate(i, 0, i))
         on(2, dose, 2)
-        on(1, st_ex, 1)
+        x_evacuate(3, 0, "vector")
         for s in range(3, 16):
+            on(s - 2, h_transpose, 0)
+            st_we(s - 3, "vector")
             on(s - 1, square, 0)
             st_yq(s - 6)
-            st_we(s - 3, "vector")
-            on(s - 2, h_transpose, 0)
             on(s - 2, times_density, 2, 3)
-            on(s - 1, square, 1)
             st_xt(s - 2)
-            on(s - 2, h_transpose, 1)
             st_q1(s - 3)
+            on(s - 1, square, 1)
             on(s - 5, st_yc)
+            st_sp(s - 0)
+            on(s - 4, st_ys)
+            on(s - 2, h_transpose, 1)
             on(s - 1, square, 2)
             st_wt(s - 2)
-            on(s - 2, lambda i: h_evacuate(i, 0, i))
-            on(s - 1, st_ex, 0)
             on(s - 0, dose, 0)
-            on(s - 4, st_ys)
-            on(s - 0, dose, 1)
-            on(s - 2, lambda i: h_evacuate(i, 1, i))
-            on(s - 0, dose, 2)
-            on(s - 3, quantize, 4, 5)
-            on(s - 3, average, 0, GV)
+            on(s - 1, st_ex, 0)
             on(s - 1, st_ex, 1)
             st_xe(s - 2, "scalar")
+            on(s - 2, lambda i: h_evacuate(i, 0, i))
+            on(s - 0, dose, 1)
+            st_se(s - 0, "vector")
+            on(s - 3, quantize, 4, 5)
+            on(s - 2, lambda i: h_evacuate(i, 1, i))
+            on(s - 0, dose, 2)
+            on(s - 3, average, 0, GV)
+        st_yq(10)
+        st_we(13, "vector")
         on(14, h_transpose, 1)
         on(15, square, 0)
-        on(15, square, 1)
-        st_yq(10)
         st_q1(13)
-        on(14, h_transpose, 0)
-        st_we(13, "vector")
         on(14, times_density, 2, 3)
-        st_wt(14)
-        on(13, quantize, 4, 5)
-        on(15, square, 2)
-        on(14, lambda i: h_evacuate(i, 0, i))
+        on(15, square, 1)
         on(15, st_ex, 0)
-        on(14, lambda i: h_evacuate(i, 1, i))
-        on(15, st_ex, 1)
-        st_we(14, "scalar")
-        on(15, h_transpose, 0)
-        on(15, h_transpose, 1)
-        on(12, st_ys)
+        on(14, h_transpose, 0)
+        on(13, quantize, 4, 5)
         st_yq(13)
-        st_q1(14)
-        y_round(11, "scalar")
+        on(15, square, 2)
+        st_wt(14)
+        on(14, lambda i: h_evacuate(i, 1, i))
         st_yq(11)
-        on(13, average, 0, GV)
-        on(15, times_density, 2, 3)
-        st_wt(15)
-        on(14, quantize, 4, 5)
-        st_we(15, "scalar")
+        on(15, h_transpose, 0)
+        on(14, lambda i: h_evacuate(i, 0, i))
+        on(12, st_ys)
+        st_q1(14)
         on(15, lambda i: h_evacuate(i, 0, i))
-        y_round(12, "scalar")
+        on(15, st_ex, 1)
+        on(15, h_transpose, 1)
+        st_we(14, "scalar")
+        y_round(11, "scalar")
+        on(15, times_density, 2, 3)
         on(15, lambda i: h_evacuate(i, 1, i))
+        on(13, average, 0, GV)
+        on(14, quantize, 4, 5)
+        st_wt(15)
         on(13, st_ys)
-        on(15, quantize, 4, 5)
+        y_round(12, "scalar")
+        st_yq(12)
         on(14, average, 0, GV)
+        st_we(15, "scalar")
         st_q1(15)
-        y_round(13, "scalar")
+        on(15, quantize, 4, 5)
         on(14, st_ys)
         st_wt(16)
-        st_yq(14)
         on(15, average, 0, GV)
-        st_wt(17)
+        st_yq(14)
+        y_round(13, "scalar")
         y_round(14, "scalar")
-        st_yq(12)
+        st_wt(17)
         st_yq(15)
-        st_we(17, "scalar")
-        on(15, st_ys)
-        st_we(16, "scalar")
         st_wt(18)
+        st_we(17, "scalar")
+        st_we(16, "scalar")
+        on(15, st_ys)
         st_wt(19)
-        st_yq(16)
         st_we(18, "scalar")
-        st_we(19, "scalar")
         st_yq(17)
+        st_yq(16)
         st_yq(18)
+        st_we(19, "scalar")
         st_yq(19)

@@ -23,14 +23,18 @@ TPP = PLANS // P
 GB = B // KP
 GV = V // KP
 LAST = TILES - 1
+XP_FROM = 7
+MU_FROM = 2
+MU_TO = 16
+XE_EVERY = 100
 YC_FROM = 13
 SPLIT = 1
-WE_FROM = 16
+WE_FROM = 13
 DX = 3
 DY = 4
 X_FROM = 7
-EVERY = 2
-YC = "vector"
+EVERY = 6
+YC = "gpsimd"
 NF = 2
 NW = 1
 D_BANKS = 4
@@ -141,7 +145,7 @@ def tile_fractionated_clonogen_survival_k7_kernel(
         def live(i):
             return 0 <= i < TILES
 
-        x_bank, x_q, h_q = {}, {}, {}
+        x_bank, x_q, h_q, x_sorted = {}, {}, {}, {}
         d_banks, squares, expo, h_bank = {}, {}, {}, {}
         y_banks, y_bf, y_src, y_grouped = {}, {}, {}, {}
         staged, codes, h_bf, word_src, halves, spread_bank = {}, {}, {}, {}, [], {}
@@ -183,9 +187,20 @@ def tile_fractionated_clonogen_survival_k7_kernel(
             for g in range(GB):
                 for u in range(2):
                     c0 = (2 * g + u) * P
-                    nc.tensor.transpose(
-                        x_bank[i][:, c0 : c0 + P], words[:, 256 * g + u : 256 * (g + 1) : 2], ident[:]
-                    )
+                    if i >= XP_FROM:
+                        src = x_sorted[i][:, c0 : c0 + P]
+                    else:
+                        src = words[:, 256 * g + u : 256 * (g + 1) : 2]
+                    nc.tensor.transpose(x_bank[i][:, c0 : c0 + P], src, ident[:])
+
+        def st_xp(k):
+            i = k + DX
+            if XP_FROM <= i < TILES:
+                x_sorted[i] = work.tile([P, KP], F32, name="x_sorted", bufs=2)
+                nc.vector.tensor_copy(
+                    out=x_sorted[i][:].rearrange("q (g u w) -> q g u w", g=GB, u=2),
+                    in_=x_sb[:, i, :].bitcast(F32).rearrange("q (g w u) -> q g u w", g=GB, u=2),
+                )
 
         def x_evacuate(i, key, engine):
             x_q[i] = key
@@ -245,7 +260,8 @@ def tile_fractionated_clonogen_survival_k7_kernel(
         def times_density(i, v0, v1):
             if v0 == NF:
                 h_bf[i] = work.tile([P, NW * KP], BF16, align_bytes=64, name="hb")
-            nc.vector.tensor_tensor(
+            engine = nc.gpsimd if MU_FROM <= i < MU_TO else nc.vector
+            engine.tensor_tensor(
                 out=word_part(h_bf[i], v0, v1, 0).rearrange("q u (w e) -> q u w e", e=2),
                 in0=word_part(expo[i], v0, v1).rearrange("q u (w e) -> q u w e", e=2),
                 in1=spread[:, i // TPP, 0:KP].rearrange("q (u w e) -> q u w e", u=2, e=2),
@@ -443,7 +459,7 @@ def tile_fractionated_clonogen_survival_k7_kernel(
 
         def st_xe(k, engine):
             if 0 < k + DX < TILES:
-                x_evacuate(k + DX, k, engine if k + DX >= X_FROM else "vector")
+                x_evacuate(k + DX, k, engine if k + DX >= X_FROM and k % XE_EVERY else "vector")
 
         def st_q1(k):
             has_x, has_h = 0 < k + DX < TILES, live(k)
@@ -503,130 +519,128 @@ def tile_fractionated_clonogen_survival_k7_kernel(
             if live(i):
                 f(i, *args)
 
+        zero_a(3)
         x_half(0, "vector")
-        x_half(1, "scalar")
         quantize(-DX, 0, 1)
+        zero_a(2)
+        x_half(1, "scalar")
         quantize(-DX, 1, 2)
+        zero_c()
         on(0, dose, 0)
         st_xt(-2)
-        zero_a(1)
-        zero_c()
-        zero_a(2)
-        zero_a(3)
-        later_loads()
         on(0, square, 0)
-        x_evacuate(1, -2, "scalar")
+        zero_a(1)
+        later_loads()
         on(0, dose, 1)
-        on(0, square, 1)
         on(0, dose, 2)
+        on(0, square, 1)
         small_bank = small_transposes()
         st_xt(-1)
+        on(0, square, 2)
+        x_evacuate(1, -2, "vector")
         on(0, st_ex, 0)
         st_q1(-2)
-        on(1, dose, 0)
         small_evacuate(small_bank)
-        x_evacuate(2, -1, "vector")
-        on(0, square, 2)
         spread_transpose(0)
-        on(1, square, 0)
-        st_q1(-1)
-        on(1, dose, 1)
-        on(1, dose, 2)
-        on(0, st_ex, 1)
         spread_evacuate(0, "vector")
-        on(1, square, 1)
-        on(2, dose, 1)
-        on(0, h_transpose, 1)
-        on(1, square, 2)
+        on(1, dose, 0)
+        x_evacuate(2, -1, "vector")
+        on(1, dose, 1)
+        on(0, st_ex, 1)
+        on(1, square, 0)
+        on(1, dose, 2)
         on(0, h_transpose, 0)
         on(0, times_density, 2, 3)
-        on(1, st_ex, 0)
-        on(1, st_ex, 1)
-        st_xt(0)
         st_wt(0)
-        on(2, dose, 0)
-        on(0, lambda i: h_evacuate(i, 1, i))
+        st_q1(-1)
+        st_xt(0)
+        on(0, h_transpose, 1)
+        on(1, square, 1)
         on(0, lambda i: h_evacuate(i, 0, i))
-        on(2, dose, 2)
+        on(2, dose, 1)
         x_evacuate(3, 0, "vector")
+        on(2, dose, 0)
+        on(1, square, 2)
+        on(0, lambda i: h_evacuate(i, 1, i))
+        st_q1(0)
+        on(1, st_ex, 0)
+        st_we(0, "vector")
+        on(1, st_ex, 1)
+        on(2, dose, 2)
+        on(2, square, 0)
+        on(1, h_transpose, 0)
         for s in range(3, 16):
-            on(s - 2, h_transpose, 0)
-            st_we(s - 3, "vector")
-            on(s - 1, square, 0)
-            st_yq(s - 6)
-            on(s - 2, times_density, 2, 3)
-            st_xt(s - 2)
-            st_q1(s - 3)
             on(s - 1, square, 1)
-            on(s - 5, st_yc)
+            on(s - 2, times_density, 2, 3)
+            on(s - 3, quantize, 4, 5)
+            on(s - 1, square, 2)
+            st_xt(s - 2)
+            on(s - 1, st_ex, 0)
             st_sp(s - 0)
+            st_wt(s - 2)
             on(s - 4, st_ys)
             on(s - 2, h_transpose, 1)
-            on(s - 1, square, 2)
-            st_wt(s - 2)
-            on(s - 0, dose, 0)
-            on(s - 1, st_ex, 0)
-            on(s - 1, st_ex, 1)
-            st_xe(s - 2, "scalar")
-            on(s - 2, lambda i: h_evacuate(i, 0, i))
-            on(s - 0, dose, 1)
             st_se(s - 0, "vector")
-            on(s - 3, quantize, 4, 5)
+            on(s - 2, lambda i: h_evacuate(i, 0, i))
+            st_xe(s - 2, "vector")
             on(s - 2, lambda i: h_evacuate(i, 1, i))
+            on(s - 5, st_yc)
+            on(s - 0, dose, 0)
+            on(s - 0, dose, 1)
+            on(s - 1, st_ex, 1)
             on(s - 0, dose, 2)
+            st_q1(s - 2)
+            st_xp(s - 0)
+            st_yq(s - 3)
             on(s - 3, average, 0, GV)
-        st_yq(10)
-        st_we(13, "vector")
-        on(14, h_transpose, 1)
-        on(15, square, 0)
-        st_q1(13)
-        on(14, times_density, 2, 3)
+            st_we(s - 2, "scalar")
+            on(s - 1, h_transpose, 0)
+            on(s - 0, square, 0)
         on(15, square, 1)
-        on(15, st_ex, 0)
-        on(14, h_transpose, 0)
+        on(14, h_transpose, 1)
         on(13, quantize, 4, 5)
-        st_yq(13)
-        on(15, square, 2)
-        st_wt(14)
-        on(14, lambda i: h_evacuate(i, 1, i))
-        st_yq(11)
-        on(15, h_transpose, 0)
-        on(14, lambda i: h_evacuate(i, 0, i))
         on(12, st_ys)
-        st_q1(14)
-        on(15, lambda i: h_evacuate(i, 0, i))
-        on(15, st_ex, 1)
-        on(15, h_transpose, 1)
-        st_we(14, "scalar")
-        y_round(11, "scalar")
-        on(15, times_density, 2, 3)
-        on(15, lambda i: h_evacuate(i, 1, i))
+        st_yq(13)
         on(13, average, 0, GV)
-        on(14, quantize, 4, 5)
-        st_wt(15)
+        on(14, times_density, 2, 3)
+        on(14, lambda i: h_evacuate(i, 0, i))
+        on(14, lambda i: h_evacuate(i, 1, i))
+        on(15, square, 2)
+        on(15, st_ex, 0)
         on(13, st_ys)
+        st_wt(14)
+        on(15, h_transpose, 0)
+        on(15, h_transpose, 1)
+        on(15, st_ex, 1)
+        st_we(14, "scalar")
+        on(15, times_density, 2, 3)
+        on(15, lambda i: h_evacuate(i, 0, i))
+        y_round(11, "scalar")
+        st_q1(14)
         y_round(12, "scalar")
-        st_yq(12)
+        on(15, lambda i: h_evacuate(i, 1, i))
+        on(14, quantize, 4, 5)
+        st_q1(15)
+        st_yq(14)
+        st_wt(15)
+        y_round(13, "scalar")
+        st_wt(16)
         on(14, average, 0, GV)
         st_we(15, "scalar")
-        st_q1(15)
         on(15, quantize, 4, 5)
         on(14, st_ys)
-        st_wt(16)
+        st_yq(15)
         on(15, average, 0, GV)
-        st_yq(14)
-        y_round(13, "scalar")
         y_round(14, "scalar")
         st_wt(17)
-        st_yq(15)
-        st_wt(18)
-        st_we(17, "scalar")
         st_we(16, "scalar")
         on(15, st_ys)
-        st_wt(19)
-        st_we(18, "scalar")
-        st_yq(17)
+        st_wt(18)
         st_yq(16)
+        st_we(17, "scalar")
+        st_wt(19)
+        st_yq(17)
+        st_we(18, "scalar")
         st_yq(18)
         st_we(19, "scalar")
         st_yq(19)

from contextlib import ExitStack

import concourse.mybir as mybir
from concourse.masks import make_identity

G, PLANS, B, V, O = 4, 512, 1024, 1536, 512
FLOPS = 2 * G * PLANS * (B * V + V * O)

F32 = mybir.dt.float32
BF16 = mybir.dt.bfloat16
I32 = mybir.dt.int32
U32 = mybir.dt.uint32
U8 = mybir.dt.uint8
FP8X4 = mybir.dt.float8_e4m3fn_x4
FP4X4 = mybir.dt.float4_e2m1fn_x4
ACT = mybir.ActivationFunctionType
ALU = mybir.AluOpType

P = 128
KP = 512
TILES = G * PLANS // P
TPP = PLANS // P
GB = B // KP
GV = V // KP
LAST = TILES - 1
XP_FROM = 7
MU_FROM = 2
MU_TO = 16
XE_EVERY = 100
YC_FROM = 13
SPLIT = 1
WE_FROM = 13
DX = 3
DY = 4
X_FROM = 7
EVERY = 6
YC = "gpsimd"
NF = 2
NW = 1
D_BANKS = 4
H_LAG = 1
Y_LAG = 4
X_STEPS = [4, 5, 6, 7, 8, 9, 10, 11, 12, 13, 14]
B_STEPS = [14]
YC_STEPS = [15]
VSQ_STEPS = []


def tile_fractionated_clonogen_survival_k7_kernel(
    tc, x, dose_words, dose_scales, density, member_words, member_scales, burden, regrowth, out_0, out_1, out_2
):
    nc = tc.nc
    x_rows = x.rearrange("j r k -> (j r) k")
    y_rows = out_0.rearrange("j r o -> (j r) o")
    out_codes = out_1[0].rearrange("p m t -> p (m t)").bitcast(I32)
    out_scales = out_2[0].bitcast(I32)

    with ExitStack() as ctx:
        keep = ctx.enter_context(tc.tile_pool(name="keep", bufs=1))
        work = ctx.enter_context(tc.tile_pool(name="work", bufs=3))
        d_psum = ctx.enter_context(tc.psum_pool(name="d_psum", bufs=D_BANKS))
        t_psum = ctx.enter_context(tc.psum_pool(name="t_psum", bufs=8 - D_BANKS))
        ctx.enter_context(tc.manual_schedule())

        x_sb = keep.tile([P, TILES, B], BF16, align_bytes=64)
        a_words = keep.tile([P, G * GB, 2 * V], U8, align_bytes=64)
        a_scales = keep.tile([P, G * GB, V], U8, align_bytes=64)
        c_words = keep.tile([P, G * GV, 2 * O], U8, align_bytes=64)
        c_scales = keep.tile([P, G * GV, O], U8, align_bytes=64)
        y_sb = keep.tile([P, TILES, O], F32, align_bytes=64)
        y_codes = keep.tile([P, TILES * P], U32, align_bytes=64)
        y_scales = keep.tile([P, TILES * P], U8, align_bytes=64)
        ident = keep.tile([P, P], F32)
        reg_raw = keep.tile([TILES, P], BF16)
        reg_rows = keep.tile([P, P], F32)
        reg = keep.tile([P, TILES], F32)
        dens_rows = keep.tile([P, KP], BF16)
        dens = keep.tile([P, G * GV, 4], BF16)
        warm = keep.tile([P, 8], F32)
        spread = keep.tile([P, G, 2 * KP], BF16, align_bytes=64)
        burd_words = keep.tile([P, 2 * G], F32)

        def zero_plane(plane):
            nc.vector.memset(plane.rearrange("p g n -> p (g n)").bitcast(I32), 0)

        def load_scales(plane, src, g0, g1):
            for q in range(4):
                nc.sync.dma_start(
                    out=plane[32 * q : 32 * q + 4, g0:g1, :].bitcast(I32),
                    in_=src[g0:g1, 4 * q : 4 * q + 4, :].rearrange("g r n -> r g n").bitcast(I32),
                )

        def load_words(tile, src, g0, g1, cols=slice(None)):
            nc.sync.dma_start(
                out=tile[:, g0:g1, cols].bitcast(I32), in_=src[g0:g1, :, cols].rearrange("g p n -> p g n").bitcast(I32)
            )

        def load_x(i0, i1):
            nc.sync.dma_start(
                out=x_sb[:, i0:i1, :], in_=x_rows[i0 * P : i1 * P, :].rearrange("(i p) k -> p i k", p=P)
            )

        zero_plane(a_scales[:, 0:GB, :])
        make_identity(nc, ident[:])
        nc.vector.memset(warm[:], 0.0)
        nc.scalar.activation(out=warm[:, 4:5], in_=warm[:, 0:1], func=ACT.Exp)
        for g in range(GB):
            nc.sync.dma_start(out=x_sb[:, 0, g * KP : (g + 1) * KP], in_=x_rows[0:P, g * KP : (g + 1) * KP])
        load_words(a_words, dose_words, 0, GB, slice(0, 2 * KP))
        load_scales(a_scales, dose_scales, 0, GB)
        load_x(1, 2)
        load_words(a_words, dose_words, 0, GB, slice(2 * KP, 2 * V))
        nc.vector.memset(dens_rows[:].bitcast(I32), 0)
        nc.vector.memset(reg_rows[:], 0.0)
        load_x(2, 4)
        nc.sync.dma_start(out=dens_rows[0 : G * GV, :], in_=density.rearrange("j (g k) -> (j g) k", k=KP))
        nc.sync.dma_start(out=reg_raw[:], in_=regrowth.rearrange("j (m p) -> (j m) p", p=P))
        nc.sync.dma_start(
            out=reg_rows[32 : 32 + 2 * G, :], in_=burden.bitcast(F32).rearrange("j (m p) -> (j m) p", p=P)
        )
        nc.gpsimd.tensor_copy(out=reg_rows[0:TILES, :], in_=reg_raw[:])
        load_x(4, 6)

        zeroed = {}

        def zero_c():
            zeroed["c"] = zero_plane(c_scales[:])

        def zero_a(j):
            zeroed[j] = zero_plane(a_scales[:, j * GB : (j + 1) * GB, :])

        def later_loads():
            assert len(zeroed) == G
            load_scales(c_scales, member_scales, 0, G * GV)
            load_scales(a_scales, dose_scales, GB, G * GB)
            load_words(c_words, member_words, 0, GV)
            load_words(a_words, dose_words, GB, 2 * GB)
            load_x(6, 8)
            load_words(c_words, member_words, GV, 2 * GV)
            for j in range(2, G):
                load_x(j * TPP, (j + 1) * TPP)
                load_words(a_words, dose_words, j * GB, (j + 1) * GB)
                load_words(c_words, member_words, j * GV, (j + 1) * GV)

        def live(i):
            return 0 <= i < TILES

        x_bank, x_q, h_q, x_sorted = {}, {}, {}, {}
        d_banks, squares, expo, h_bank = {}, {}, {}, {}
        y_banks, y_bf, y_src, y_grouped = {}, {}, {}, {}
        staged, codes, h_bf, word_src, halves, spread_bank = {}, {}, {}, {}, [], {}

        def new_t_bank():
            return t_psum.tile([P, KP], F32, name="t_bank")

        def copy_on(engine, dst, src):
            if engine == "scalar":
                nc.scalar.copy(out=dst, in_=src)
            elif engine == "gpsimd":
                nc.gpsimd.tensor_scalar(out=dst, in0=src, scalar1=1.0, scalar2=1.0, op0=ALU.mult, op1=ALU.mult)
            else:
                nc.vector.tensor_copy(out=dst, in_=src)

        def evacuate(engine, dst_words, bank):
            src = bank.rearrange("p (a u c) -> p a c u", u=2, c=P)
            copy_on(engine, dst_words.rearrange("p (a c u) -> p a c u", u=2, c=P), src)

        def stage(key):
            if key not in staged:
                staged[key] = work.tile([P, B + V + O], BF16, align_bytes=64, name="staged", bufs=4)
                qc = work.tile([P, (GB + GV) * P], U32, align_bytes=64, name="qc", bufs=4)
                qs = work.tile([P, (GB + GV) * P], U8, align_bytes=64, name="qs", bufs=4)
                codes[key] = (qc, qs)
            return staged[key]

        def quantize(key, g0, g1):
            qc, qs = codes[key]
            nc.vector.quantize_mx(
                out=qc[:, g0 * P : g1 * P].bitcast(FP8X4),
                scales=qs[:, g0 * P : g1 * P],
                in_=staged[key][:, g0 * KP : g1 * KP],
            )

        def x_transpose(i):
            x_bank[i] = new_t_bank()
            words = x_sb[:, i, :].bitcast(F32)
            for g in range(GB):
                for u in range(2):
                    c0 = (2 * g + u) * P
                    if i >= XP_FROM:
                        src = x_sorted[i][:, c0 : c0 + P]
                    else:
                        src = words[:, 256 * g + u : 256 * (g + 1) : 2]
                    nc.tensor.transpose(x_bank[i][:, c0 : c0 + P], src, ident[:])

        def st_xp(k):
            i = k + DX
            if XP_FROM <= i < TILES:
                x_sorted[i] = work.tile([P, KP], F32, name="x_sorted", bufs=2)
                nc.vector.tensor_copy(
                    out=x_sorted[i][:].rearrange("q (g u w) -> q g u w", g=GB, u=2),
                    in_=x_sb[:, i, :].bitcast(F32).rearrange("q (g w u) -> q g u w", g=GB, u=2),
                )

        def x_evacuate(i, key, engine):
            x_q[i] = key
            evacuate(engine, stage(key)[:, 0:B].bitcast(F32), x_bank[i][:])

        def dose(i, vg):
            j = i // TPP
            qc, qs = codes[x_q[i]]
            d_banks[i, vg] = d_psum.tile([P, KP], F32, name="d_bank")
            for g in range(GB):
                nc.tensor.matmul_mx(
                    out=d_banks[i, vg][:],
                    lhsT=qc[:, g * P : (g + 1) * P].bitcast(FP8X4),
                    lhsT_scale=qs[:, g * P : (g + 1) * P],
                    rhs=a_words[:, j * GB + g, vg * 2 * KP : (vg + 1) * 2 * KP].bitcast(FP4X4),
                    rhs_scale=a_scales[:, j * GB + g, vg * KP : (vg + 1) * KP],
                    start=(g == 0),
                    stop=(g == GB - 1),
                )

        def word_part(tile, v0, v1, first=NF * KP):
            return tile[:, first:].rearrange("q (u c) -> q u c", u=2)[:, :, (v0 - NF) * 256 : (v1 - NF) * 256]

        def square(i, vg):
            if vg == 0:
                squares[i] = work.tile([P, V], F32, name="sq", bufs=2)
            if vg < NF:
                dst = squares[i][:, vg * KP : (vg + 1) * KP].rearrange("q (t p) -> q t p", t=4)
                src = d_banks[i, vg][:].rearrange("q (p t) -> q t p", t=4)
            else:
                dst = word_part(squares[i], vg, vg + 1).rearrange("q u (w e) -> q u w e", e=2)
                src = d_banks[i, vg][:].rearrange("q (w u e) -> q u w e", u=2, e=2)
            nc.scalar.activation(out=dst, in_=src, func=ACT.Square, bias=2.5)

        def vector_square(i, vg):
            shifted = work.tile([P, KP], F32, name="shifted", bufs=1)
            nc.vector.tensor_scalar(
                out=shifted[:].rearrange("q (t p) -> q t p", t=4),
                in0=d_banks[i, vg][:].rearrange("q (p t) -> q t p", t=4),
                scalar1=2.5,
                scalar2=None,
                op0=ALU.add,
            )
            nc.vector.tensor_tensor(
                out=squares[i][:, vg * KP : (vg + 1) * KP], in0=shifted[:], in1=shifted[:], op=ALU.mult
            )

        def exponential(i, v0, v1):
            if v0 == 0:
                expo[i] = work.tile([P, V], F32, name="ex", bufs=3)
            if v1 <= NF or v1 == GV and v0 <= NF:
                dst, src = expo[i][:, v0 * KP : v1 * KP], squares[i][:, v0 * KP : v1 * KP]
            else:
                dst, src = word_part(expo[i], v0, v1), word_part(squares[i], v0, v1)
            nc.scalar.activation(out=dst, in_=src, func=ACT.Exp, bias=0.9375, scale=-0.15)

        def times_density(i, v0, v1):
            if v0 == NF:
                h_bf[i] = work.tile([P, NW * KP], BF16, align_bytes=64, name="hb")
            engine = nc.gpsimd if MU_FROM <= i < MU_TO else nc.vector
            engine.tensor_tensor(
                out=word_part(h_bf[i], v0, v1, 0).rearrange("q u (w e) -> q u w e", e=2),
                in0=word_part(expo[i], v0, v1).rearrange("q u (w e) -> q u w e", e=2),
                in1=spread[:, i // TPP, 0:KP].rearrange("q (u w e) -> q u w e", u=2, e=2),
                op=ALU.mult,
            )

        def half_bank():
            if not halves:
                bank = new_t_bank()
                halves.extend([(bank, 1), (bank, 0)])
            return halves.pop()

        def word_transpose(name, words):
            bank, slot = half_bank()
            word_src[name] = (bank, slot)
            for u in range(2):
                c0 = (2 * slot + u) * P
                nc.tensor.transpose(bank[:, c0 : c0 + P], words[:, u, :], ident[:])

        def hw_transpose(i, vg):
            word_transpose(("h", i, vg), word_part(h_bf[i], vg, vg + 1, 0).bitcast(F32))

        def yw_transpose(i):
            word_transpose(("y", i), y_bf[i][:].bitcast(F32))

        def word_evacuate(name, n, key, col, engine):
            bank, slot = word_src[name]
            evacuate(
                engine, stage(key)[:, col : col + n * KP].bitcast(F32), bank[:, slot * 256 : (slot + n) * 256]
            )

        def hw_evacuate(i, vg, n, key, engine):
            h_q[i] = key
            word_evacuate(("h", i, vg), n, key, B + vg * KP, engine)

        def yw_evacuate(i, key, engine):
            word_evacuate(("y", i), 1, key, B + V, engine)

        def yw_quantize(i, key):
            cols = slice(i * P, (i + 1) * P)
            nc.vector.quantize_mx(
                out=y_codes[:, cols].bitcast(FP8X4), scales=y_scales[:, cols], in_=staged[key][:, B + V :]
            )

        def h_transpose(i, vg):
            h_bank[i, vg] = new_t_bank()
            for t in range(4):
                c0 = vg * KP + t * P
                nc.tensor.transpose(h_bank[i, vg][:, t * P : (t + 1) * P], expo[i][:, c0 : c0 + P], ident[:])

        def h_evacuate(i, vg, key):
            h_q[i] = key
            k = (i // TPP) * GV + vg
            nc.vector.tensor_tensor(
                out=stage(key)[:, B + vg * KP : B + (vg + 1) * KP].rearrange("p (c t) -> p c t", t=4),
                in0=h_bank[i, vg][:].rearrange("p (t c) -> p c t", t=4),
                in1=dens[:, k : k + 1, :].to_broadcast([P, P, 4]),
                op=ALU.mult,
            )

        def average(i, v0, v1):
            j = i // TPP
            qc, qs = codes[h_q[i]]
            if v0 == 0:
                y_banks[i] = d_psum.tile([P, O], F32, name="d_bank")
            for vg in range(v0, v1):
                cols = slice((GB + vg) * P, (GB + vg + 1) * P)
                nc.tensor.matmul_mx(
                    out=y_banks[i][:],
                    lhsT=qc[:, cols].bitcast(FP8X4),
                    lhsT_scale=qs[:, cols],
                    rhs=c_words[:, j * GV + vg, :].bitcast(FP4X4),
                    rhs_scale=c_scales[:, j * GV + vg, :],
                    start=(vg == 0),
                    stop=(vg == GV - 1),
                )

        def y_scale(i):
            j = i // TPP
            nc.vector.scalar_tensor_tensor(
                out=y_sb[:, i, :],
                in0=y_banks[i][:],
                scalar=reg[:, i : i + 1],
                in1=spread[:, j, KP:],
                op0=ALU.mult,
                op1=ALU.mult,
            )
            nc.sync.dma_start(out=y_rows[i * P : (i + 1) * P, :], in_=y_sb[:, i, :])

        def y_round(i, engine):
            y_bf[i] = work.tile([P, 2, 256], BF16, align_bytes=64, name="yb", bufs=4)
            copy_on(
                engine,
                y_bf[i][:].rearrange("q u (w e) -> q u w e", e=2),
                y_sb[:, i, :].rearrange("q (w u e) -> q u w e", u=2, e=2),
            )

        def y_scale_round(i):
            j = i // TPP
            y_bf[i] = work.tile([P, 2, 256], BF16, align_bytes=64, name="yb", bufs=4)
            for u in range(2):
                nc.vector.scalar_tensor_tensor(
                    out=y_bf[i][:, u, :].rearrange("q (w e) -> q w e", e=2),
                    in0=y_banks[i][:].rearrange("q (w u e) -> q u w e", u=2, e=2)[:, u],
                    scalar=reg[:, i : i + 1],
                    in1=spread[:, j, KP:].rearrange("q (w u e) -> q u w e", u=2, e=2)[:, u],
                    op0=ALU.mult,
                    op1=ALU.mult,
                )

        def x_half(g, engine):
            bank = new_t_bank()
            words = x_sb[:, 0, :].bitcast(F32)
            for u in range(2):
                nc.tensor.transpose(bank[:, u * P : (u + 1) * P], words[:, 256 * g + u : 256 * (g + 1) : 2], ident[:])
            x_q[0] = -DX
            evacuate(engine, stage(-DX)[:, g * KP : (g + 1) * KP].bitcast(F32), bank[:, 0:256])

        def y_transpose(i0, i1):
            bank = new_t_bank()
            y_src[i0] = bank
            for i in range(i0, i1):
                for u in range(2):
                    c0 = (2 * (i - i0) + u) * P
                    nc.tensor.transpose(bank[:, c0 : c0 + P], y_bf[i][:, u, :].bitcast(F32), ident[:])

        def y_evacuate(i0, i1, engine):
            y_grouped[i0] = work.tile([P, 2 * O], BF16, align_bytes=64, name="yg")
            n = (i1 - i0) * 256
            evacuate(engine, y_grouped[i0][:].bitcast(F32)[:, 0:n], y_src[i0][:, 0:n])

        def y_quantize(i0, i1):
            cols = slice(i0 * P, i1 * P)
            nc.vector.quantize_mx(
                out=y_codes[:, cols].bitcast(FP8X4), scales=y_scales[:, cols], in_=y_grouped[i0][:, 0 : (i1 - i0) * O]
            )

        def store_planes(i0, i1):
            cols = slice(i0 * P, i1 * P)
            nc.sync.dma_start(out=out_codes[:, cols], in_=y_codes[:, cols].bitcast(I32))

        def store_scales(i0, i1, queues):
            for q in range(4):
                queues[q % len(queues)].dma_start(
                    out=out_scales[4 * q : 4 * q + 4, i0 * 32 : i1 * 32],
                    in_=y_scales[32 * q : 32 * q + 4, i0 * P : i1 * P].bitcast(I32),
                )

        def small_transposes():
            bank = new_t_bank()
            words = dens_rows[:].bitcast(F32)
            for u in range(2):
                nc.tensor.transpose(bank[:, u * P : (u + 1) * P], words[:, u : 256 : 2], ident[:])
            nc.tensor.transpose(bank[:, 2 * P : 3 * P], reg_rows[:], ident[:])
            return bank

        def small_evacuate(bank):
            nc.vector.tensor_copy(
                out=dens[:].rearrange("p k t -> p (k t)").bitcast(F32).rearrange("p (k u) -> p k u", u=2),
                in_=bank[:, 0 : 2 * P].rearrange("p (u c) -> p c u", u=2)[:, 0 : G * GV, :],
            )
            nc.vector.tensor_copy(out=reg[:], in_=bank[:, 2 * P : 2 * P + TILES])
            nc.vector.tensor_copy(out=burd_words[:], in_=bank[:, 2 * P + 32 : 2 * P + 32 + 2 * G])

        def spread_transpose(j):
            spread_bank[j] = d_psum.tile([P, KP], F32, name="d_bank")
            dens_words = dens[:].rearrange("p k t -> p (k t)").bitcast(F32)
            for u in range(2):
                c = 2 * (j * GV + GV - 1) + u
                nc.tensor.transpose(
                    spread_bank[j][:, u * P : (u + 1) * P], dens_words[:, c : c + 1].to_broadcast([P, P]), ident[:]
                )
            for m in range(2):
                c = 2 * j + m
                nc.tensor.transpose(
                    spread_bank[j][:, (2 + m) * P : (3 + m) * P],
                    burd_words[:, c : c + 1].to_broadcast([P, P]),
                    ident[:],
                )

        def spread_evacuate(j, engine):
            copy_on(engine, spread[:, j, :].bitcast(F32), spread_bank[j][:])

        def st_sp(s):
            if s % TPP == 0 and 0 < s // TPP < G:
                spread_transpose(s // TPP)

        def st_se(s, engine):
            if s % TPP == 0 and 0 < s // TPP < G:
                spread_evacuate(s // TPP, engine)

        def st_xt(k):
            if 0 < k + DX < TILES:
                x_transpose(k + DX)

        def st_xe(k, engine):
            if 0 < k + DX < TILES:
                x_evacuate(k + DX, k, engine if k + DX >= X_FROM and k % XE_EVERY else "vector")

        def st_q1(k):
            has_x, has_h = 0 < k + DX < TILES, live(k)
            if has_x or has_h:
                quantize(k, 0 if has_x else 2, 4 if has_h else 2)

        def st_wt(k):
            halves.clear()
            if live(k):
                hw_transpose(k, 2)
            elif live(k - DY):
                half_bank_skip()
            if live(k - DY):
                yw_transpose(k - DY)

        def half_bank_skip():
            half_bank()

        def st_we(k, engine):
            if k < 13 and (k % EVERY == 0 or k >= WE_FROM):
                engine = "scalar"
            if live(k):
                hw_evacuate(k, 2, 2 if live(k - DY) else 1, k, engine)
            elif live(k - DY):
                yw_evacuate(k - DY, k, engine)

        def st_yq(k):
            i = k - DY
            if live(i):
                yw_quantize(i, k)
                if i == LAST - 1:
                    store_planes(LAST + 1 - TPP, LAST)
                elif i == LAST:
                    store_planes(LAST, TILES)
                    store_scales(LAST + 1 - TPP, TILES, [nc.scalar, nc.sync])
                elif i % TPP == TPP - 1:
                    store_planes(i + 1 - TPP, i + 1)
                if i == LAST - TPP:
                    store_scales(0, i + 1, [nc.sync])

        def st_ys(i):
            if i == LAST:
                y_scale_round(i)
            y_scale(i)

        def st_yc(i):
            if i < LAST:
                y_round(i, "scalar" if i >= YC_FROM else YC)

        def st_ex(i, part):
            if i == 0 or i == LAST or SPLIT:
                exponential(i, 2 * part, 2 + part)
            elif part == 1:
                exponential(i, 0, 3)

        def on(i, f, *args):
            if live(i):
                f(i, *args)

        zero_a(3)
        x_half(0, "vector")
        quantize(-DX, 0, 1)
        zero_a(2)
        x_half(1, "scalar")
        quantize(-DX, 1, 2)
        zero_c()
        on(0, dose, 0)
        st_xt(-2)
        on(0, square, 0)
        zero_a(1)
        later_loads()
        on(0, dose, 1)
        on(0, dose, 2)
        on(0, square, 1)
        small_bank = small_transposes()
        st_xt(-1)
        on(0, square, 2)
        x_evacuate(1, -2, "vector")
        on(0, st_ex, 0)
        st_q1(-2)
        small_evacuate(small_bank)
        spread_transpose(0)
        spread_evacuate(0, "vector")
        on(1, dose, 0)
        x_evacuate(2, -1, "vector")
        on(1, dose, 1)
        on(0, st_ex, 1)
        on(1, square, 0)
        on(1, dose, 2)
        on(0, h_transpose, 0)
        on(0, times_density, 2, 3)
        st_wt(0)
        st_q1(-1)
        st_xt(0)
        on(0, h_transpose, 1)
        on(1, square, 1)
        on(0, lambda i: h_evacuate(i, 0, i))
        on(2, dose, 1)
        x_evacuate(3, 0, "vector")
        on(2, dose, 0)
        on(1, square, 2)
        on(0, lambda i: h_evacuate(i, 1, i))
        st_q1(0)
        on(1, st_ex, 0)
        st_we(0, "vector")
        on(1, st_ex, 1)
        on(2, dose, 2)
        on(2, square, 0)
        on(1, h_transpose, 0)
        for s in range(3, 16):
            on(s - 1, square, 1)
            on(s - 2, times_density, 2, 3)
            on(s - 3, quantize, 4, 5)
            on(s - 1, square, 2)
            st_xt(s - 2)
            on(s - 1, st_ex, 0)
            st_sp(s - 0)
            st_wt(s - 2)
            on(s - 4, st_ys)
            on(s - 2, h_transpose, 1)
            st_se(s - 0, "vector")
            on(s - 2, lambda i: h_evacuate(i, 0, i))
            st_xe(s - 2, "vector")
            on(s - 2, lambda i: h_evacuate(i, 1, i))
            on(s - 5, st_yc)
            on(s - 0, dose, 0)
            on(s - 0, dose, 1)
            on(s - 1, st_ex, 1)
            on(s - 0, dose, 2)
            st_q1(s - 2)
            st_xp(s - 0)
            st_yq(s - 3)
            on(s - 3, average, 0, GV)
            st_we(s - 2, "scalar")
            on(s - 1, h_transpose, 0)
            on(s - 0, square, 0)
        on(15, square, 1)
        on(14, h_transpose, 1)
        on(13, quantize, 4, 5)
        on(12, st_ys)
        st_yq(13)
        on(13, average, 0, GV)
        on(14, times_density, 2, 3)
        on(14, lambda i: h_evacuate(i, 0, i))
        on(14, lambda i: h_evacuate(i, 1, i))
        on(15, square, 2)
        on(15, st_ex, 0)
        on(13, st_ys)
        st_wt(14)
        on(15, h_transpose, 0)
        on(15, h_transpose, 1)
        on(15, st_ex, 1)
        st_we(14, "scalar")
        on(15, times_density, 2, 3)
        on(15, lambda i: h_evacuate(i, 0, i))
        y_round(11, "scalar")
        st_q1(14)
        y_round(12, "scalar")
        on(15, lambda i: h_evacuate(i, 1, i))
        on(14, quantize, 4, 5)
        st_q1(15)
        st_yq(14)
        st_wt(15)
        y_round(13, "scalar")
        st_wt(16)
        on(14, average, 0, GV)
        st_we(15, "scalar")
        on(15, quantize, 4, 5)
        on(14, st_ys)
        st_yq(15)
        on(15, average, 0, GV)
        y_round(14, "scalar")
        st_wt(17)
        st_we(16, "scalar")
        on(15, st_ys)
        st_wt(18)
        st_yq(16)
        st_we(17, "scalar")
        st_wt(19)
        st_yq(17)
        st_we(18, "scalar")
        st_yq(18)
        st_we(19, "scalar")
        st_yq(19)
